import numpy as np
import ml_dtypes


def mxq(x, axis, fmt="e4m3"):
    dtype, down = {"e4m3": (ml_dtypes.float8_e4m3fn, 7), "e5m2": (ml_dtypes.float8_e5m2, 14)}[fmt]
    v = np.moveaxis(np.asarray(x, np.float32).astype(ml_dtypes.bfloat16).astype(np.float64), axis, -1)
    blocks = v.reshape(v.shape[:-1] + (-1, 32))
    amax = np.abs(blocks).max(-1, keepdims=True)
    byte = np.maximum(np.where(amax > 0, np.frexp(amax)[1] - 1 + 127, 0) - down, 1)
    scale = np.exp2(byte - 127.0)
    codes = (blocks / scale).astype(np.float32).astype(dtype).astype(np.float64)
    return np.moveaxis((codes * scale).reshape(v.shape), -1, axis)


WIDE = False


def mx_kscale(k):
    if not WIDE:
        return np.ones(k)
    levels = np.array([10, -10, 5, -5, 0])
    if k % 512:
        return np.exp2(np.random.permutation(np.resize(levels, k // 32))).repeat(32)
    a = np.empty((k // 512, 16))
    for p in range(k // 512):
        a[p, :8] = np.random.permutation(np.resize(levels, 8))
        for g in range(8):
            far = levels[np.abs(levels - a[p, g]) >= 10]
            a[p, g + 8] = far[np.random.randint(len(far))]
    return np.exp2(a.ravel()).repeat(32)


def f64(x):
    return np.asarray(x).astype(np.float64)


def striped(idx):
    return np.tile(idx.reshape(-1, 16).T, (8, 1)).astype(np.uint16)


def unstriped(offs):
    return offs[:16].T.reshape(-1).astype(np.int64)


def pack_weight(w):
    k, n = w.shape
    w = f64(np.asarray(w, np.float32).astype(ml_dtypes.bfloat16)).reshape(k // 32, 32, n)
    amax = np.abs(w).max(1)
    byte = np.clip(np.where(amax > 0, np.frexp(amax)[1] - 1 + 127 - 7, 1), 1, 254)
    scaled = (w * np.exp2(127.0 - byte)[:, None, :]).reshape(k, n).astype(np.float32)
    words = np.ascontiguousarray(scaled.reshape(k // 512, 128, 4, n).transpose(0, 1, 3, 2)).astype(ml_dtypes.float8_e4m3fn).view(np.uint8)
    return words, np.ascontiguousarray(byte.astype(np.uint8).reshape(k // 512, 16, n))


def unpack_weight(words, scales):
    g, p, n, _ = words.shape
    vals = np.ascontiguousarray(words).view(ml_dtypes.float8_e4m3fn).astype(np.float64) * np.repeat(np.exp2(scales.astype(np.float64) - 127.0), 8, axis=1)[..., None]
    return vals.transpose(0, 1, 3, 2).reshape(g * 512, n)


def planes(y):
    n, m = y.shape
    v = y.astype(np.float32).astype(ml_dtypes.bfloat16).astype(np.float64).reshape(n // 32, 32, m)
    top = np.abs(v).max(1)
    byte = np.clip(np.where(top > 0, np.frexp(top)[1] - 1 + 127 - 7, 1), 1, 254)
    codes = (v * np.exp2(127.0 - byte)[:, None, :]).reshape(n, m).astype(np.float32).astype(ml_dtypes.float8_e4m3fn).view(np.uint8)
    words = codes.reshape(n // 512, 128, 4, m).transpose(0, 1, 3, 2)
    return np.ascontiguousarray(words), np.ascontiguousarray(byte.astype(np.uint8).reshape(n // 512, 16, m))


def relu(v):
    return np.maximum(v, 0.0)


K, T, S, H, N, V = 512, 2048, 512, 512, 512, 256
P = 2 ** 7


def setup_inputs():
    n = np.random.standard_normal
    s = mx_kscale(K)[:, None]
    u = mx_kscale(H)
    packed_xT = pack_weight(n((K, T)) * s)
    return {
        "x_words": packed_xT[0],
        "x_scales": packed_xT[1],
        "w1": (n((K, H)) / np.sqrt(K) / s * u).astype(np.float32),
        "w2": (n((H, N)) / np.sqrt(H) / u[:, None]).astype(np.float32),
        "w3": (n((K, N)) / np.sqrt(K) / s).astype(np.float32),
        "score": (np.tile(np.random.uniform(0.2, 1.0, S), (P, 1))).astype(np.float32),
        "offs": striped(np.random.permutation(T)[:S]),
        "kept": striped(np.random.permutation(S)[:V]),
    }


def reference(x_words, x_scales, w1, w2, w3, score, offs, kept):
    xq = unpack_weight(x_words, x_scales)[:, unstriped(offs)]
    h = relu(mxq(f64(w1), 0, "e4m3").T @ xq)
    z = h[:, unstriped(kept)] * (f64(score)[:1][:, unstriped(kept)])
    rr = mxq(f64(w2), 0, "e4m3").T @ mxq(z, 0, "e4m3")
    up = np.zeros((H, S))
    up[:, unstriped(kept)] = rr
    y = mxq(f64(w3), 0, "e4m3").T @ xq
    out_0 = up + y
    return (out_0,) + planes(out_0)

@@ -1,0 +1,208 @@
+from contextlib import ExitStack
+
+import concourse.mybir as mybir
+
+K, T, S, H, N, V = 512, 2048, 512, 512, 512, 256
+FLOPS = 2 * K * H * S + 2 * H * N * V + 2 * K * N * S
+
+F32 = mybir.dt.float32
+BF16 = mybir.dt.bfloat16
+I32 = mybir.dt.int32
+U32 = mybir.dt.uint32
+U16 = mybir.dt.uint16
+U8 = mybir.dt.uint8
+FP8X4 = mybir.dt.float8_e4m3fn_x4
+RELU = mybir.ActivationFunctionType.Relu
+MULT = mybir.AluOpType.mult
+ADD = mybir.AluOpType.add
+
+P = 128
+PACK = 4
+HALF = S // 2
+
+
+def tile_picked_ygunet_none_po_kernel(
+    tc, x_words, x_scales, w1, w2, w3, score, offs, kept, out_0, out_1, out_2
+):
+    nc = tc.nc
+    with ExitStack() as ctx:
+        sb = ctx.enter_context(tc.tile_pool(name="sb", bufs=1))
+        ps = ctx.enter_context(tc.psum_pool(name="ps", bufs=1))
+
+        def sbuf(name, shape, dtype):
+            return sb.tile(shape, dtype, name=name, align_bytes=64)
+
+
+        def load_weight(name, w, tag):
+            raw = sb.tile([P, PACK, 512], F32, name=name + "_raw", tag=tag, align_bytes=64)
+            nc.sync.dma_start(out=raw[:], in_=w.rearrange("(p j) c -> p j c", j=PACK))
+            return raw
+
+        def round_pair(name, raw, pair, copy):
+            grouped = sbuf("%s_grouped%d" % (name, pair), [P, 2, P, PACK], BF16)
+            src = raw[:].rearrange("p j (m t) -> p m j t", t=PACK)[:, :, :, 2 * pair : 2 * pair + 2]
+            copy(out=grouped[:].rearrange("p t m j -> p m j t"), in_=src)
+            return grouped
+
+        def quantize_pair(name, grouped, pair):
+            codes = sbuf("%s_codes%d" % (name, pair), [P, 2 * P], U32)
+            scales = sbuf("%s_scales%d" % (name, pair), [P, 2 * P], U8)
+            nc.vector.quantize_mx(
+                out=codes[:].bitcast(FP8X4), scales=scales[:], in_=grouped[:].rearrange("p t m j -> p (t m j)")
+            )
+            return codes, scales
+
+        def product(bank, weight, t, codes, scales):
+            w_codes, w_scales = weight[t // 2]
+            cols = slice((t % 2) * P, (t % 2 + 1) * P)
+            nc.tensor.matmul_mx(
+                out=bank,
+                lhsT=w_codes[:, cols].bitcast(FP8X4),
+                lhsT_scale=w_scales[:, cols],
+                rhs=codes.bitcast(FP8X4),
+                rhs_scale=scales,
+                start=True,
+                stop=True,
+            )
+
+        def interleave(copy, dst, src):
+            copy(out=dst.rearrange("p (c i) t -> p c t i", i=4), in_=src.rearrange("p t (c i) -> p c t i", i=4))
+
+        xs_all = sbuf("xs_all", [P, T], U8)
+        nc.vector.memset(xs_all[:].bitcast(I32), 0)
+        offs_sb = sbuf("offs_sb", [P, S // 16], U16)
+        nc.sync.dma_start(offs_sb[:], offs)
+        kept_sb = sbuf("kept_sb", [P, V // 16], U16)
+        nc.sync.dma_start(kept_sb[:], kept)
+        w1_raw = load_weight("w1", w1, "stage_a")
+        for q in range(4):
+            nc.scalar.dma_start(
+                out=xs_all[32 * q : 32 * q + 4, :].bitcast(I32), in_=x_scales[0, 4 * q : 4 * q + 4, :].bitcast(I32)
+            )
+        xw_all = sbuf("xw_all", [P, T], I32)
+        nc.sync.dma_start(out=xw_all[:], in_=x_words[0].rearrange("p n t -> p (n t)").bitcast(I32))
+        score_sb = sbuf("score_sb", [P, S], F32)
+        nc.sync.dma_start(out=score_sb[:], in_=score)
+        w2_raw = load_weight("w2", w2, "stage_b")
+
+        up = [sbuf("up%d" % t, [P, S], F32) for t in range(PACK)]
+        for t in range(PACK):
+            nc.vector.memset(up[t][:], 0.0)
+        warm = sbuf("warm", [P, 1], F32)
+        nc.scalar.activation(warm[:], up[0][:, 0:1], RELU)
+
+        xs = sbuf("xs", [P, S], U8)
+        nc.vector.tensor_copy(xs[:], xs_all[:].indirect(offs_sb[:]))
+        w1_g = [round_pair("w1", w1_raw, pair, nc.scalar.copy) for pair in range(2)]
+        w3_raw = load_weight("w3", w3, "stage_a")
+        w1_q = [quantize_pair("w1", w1_g[0], 0)]
+        halves = [slice(0, HALF), slice(HALF, S)]
+        xw = sbuf("xw", [P, S], U32)
+        for i in range(2):
+            entries = offs_sb[:, i * (HALF // 16) : (i + 1) * (HALF // 16)]
+            nc.vector.tensor_copy(xw[:, halves[i]], xw_all[:].bitcast(U32).indirect(entries))
+        w1_q.append(quantize_pair("w1", w1_g[1], 1))
+        score_kept = sbuf("score_kept", [P, V], F32)
+        nc.vector.tensor_copy(score_kept[:], score_sb[:].indirect(kept_sb[:]))
+
+        z = sbuf("z", [P, PACK, V], F32)
+        h = [sbuf("h%d" % t, [P, S], F32) for t in range(PACK)]
+
+        def hidden(t, i):
+            h_ps = ps.tile([P, HALF], F32, name="h_ps", tag="bank%d" % (2 * t + i))
+            product(h_ps[:], w1_q, t, xw[:, halves[i]], xs[:, halves[i]])
+            nc.scalar.activation(h[t][:, halves[i]], h_ps[:], RELU)
+
+        def weigh(t):
+            nc.vector.tensor_tensor(z[:, t, :], h[t][:].indirect(kept_sb[:]), score_kept[:], MULT)
+
+        hidden(0, 0)
+        hidden(1, 0)
+        hidden(0, 1)
+        weigh(0)
+        hidden(1, 1)
+        weigh(1)
+        for t in (2, 3):
+            hidden(t, 0)
+            hidden(t, 1)
+            weigh(t)
+        w2_g = [round_pair("w2", w2_raw, pair, nc.scalar.copy) for pair in range(2)]
+        z_grouped = sbuf("z_grouped", [P, V, PACK], BF16)
+        z_codes = sbuf("z_codes", [P, V], U32)
+        z_scales = sbuf("z_scales", [P, V], U8)
+        z_halves = [slice(0, V // 2), slice(V // 2, V)]
+
+        def quantize_z(cols):
+            nc.vector.quantize_mx(
+                out=z_codes[:, cols].bitcast(FP8X4),
+                scales=z_scales[:, cols],
+                in_=z_grouped[:, cols, :].rearrange("p v t -> p (v t)"),
+            )
+
+        interleave(nc.vector.tensor_copy, z_grouped[:, z_halves[0], :], z[:, :, z_halves[0]])
+        w2_q = [quantize_pair("w2", w2_g[0], 0)]
+        quantize_z(z_halves[0])
+        interleave(nc.vector.tensor_copy, z_grouped[:, z_halves[1], :], z[:, :, z_halves[1]])
+        quantize_z(z_halves[1])
+        w2_q.append(quantize_pair("w2", w2_g[1], 1))
+
+        result = sbuf("result", [P, PACK, S], F32)
+        out_rows = out_0.rearrange("(p t) n -> p t n", t=PACK)
+        y_ps = {}
+
+        def scatter(t, cols, bank):
+            width = cols.stop - cols.start
+            rr_ps = ps.tile([P, width], F32, name="rr_ps", tag="bank%d" % bank)
+            product(rr_ps[:], w2_q, t, z_codes[:, cols], z_scales[:, cols])
+            rr = sbuf("rr%d_%d" % (t, cols.start), [P, width], F32)
+            nc.scalar.copy(rr[:], rr_ps[:])
+            nc.vector.tensor_copy(up[t][:].indirect(kept_sb[:, cols.start // 16 : cols.stop // 16]), rr[:])
+
+        def skip(t):
+            y_ps[t] = ps.tile([P, S], F32, name="y_ps", tag="bank%d" % (4 + t))
+            product(y_ps[t][:], w3_q, t, xw[:], xs[:])
+
+        def add(t, cols):
+            nc.vector.tensor_tensor(result[:, t, cols], up[t][:, cols], y_ps[t][:, cols], ADD)
+
+        whole = slice(0, S)
+        scatter(0, z_halves[0], 0)
+        scatter(0, z_halves[1], 1)
+        w3_g = [round_pair("w3", w3_raw, 0, nc.scalar.copy)]
+        w3_q = [quantize_pair("w3", w3_g[0], 0)]
+        skip(0)
+        skip(1)
+        scatter(1, slice(0, V), 2)
+        w3_g.append(round_pair("w3", w3_raw, 1, nc.scalar.copy))
+        for t in range(2):
+            add(t, whole)
+            nc.sync.dma_start(out=out_rows[:, t, :], in_=result[:, t, :])
+        w3_q.append(quantize_pair("w3", w3_g[1], 1))
+        skip(2)
+        skip(3)
+        scatter(2, slice(0, V), 3)
+        add(2, whole)
+        nc.sync.dma_start(out=out_rows[:, 2, :], in_=result[:, 2, :])
+        scatter(3, slice(0, V), 0)
+        add(3, halves[0])
+        add(3, halves[1])
+        nc.sync.dma_start(out=out_rows[:, 3, :], in_=result[:, 3, :])
+
+        o_scales = sbuf("o_scales", [P, S], U8)
+        words = out_1[0].rearrange("p n t -> p (n t)").bitcast(I32)
+        o_grouped = [sbuf("o_grouped%d" % i, [P, HALF, PACK], BF16) for i in range(2)]
+        interleave(nc.scalar.copy, o_grouped[0][:], result[:, :, halves[0]])
+        interleave(nc.vector.tensor_copy, o_grouped[1][:], result[:, :, halves[1]])
+        for i in (1, 0):
+            o_codes = sbuf("o_codes%d" % i, [P, HALF], I32)
+            nc.vector.quantize_mx(
+                out=o_codes[:].bitcast(FP8X4),
+                scales=o_scales[:, halves[i]],
+                in_=o_grouped[i][:].rearrange("p n t -> p (n t)"),
+            )
+            nc.sync.dma_start(out=words[:, halves[i]], in_=o_codes[:])
+        for q in range(4):
+            queue = nc.scalar if q % 2 == 0 else nc.sync
+            queue.dma_start(
+                out=out_2[0, 4 * q : 4 * q + 4, :].bitcast(I32), in_=o_scales[32 * q : 32 * q + 4, :].bitcast(I32)
+            )

@@ -29,8 +29,15 @@ def tile_picked_ygunet_none_po_kernel(
         sb = ctx.enter_context(tc.tile_pool(name="sb", bufs=1))
         ps = ctx.enter_context(tc.psum_pool(name="ps", bufs=1))
 
+        shared = {
+            "w2_grouped0": "w1_codes1",
+            "w2_grouped1": "w1_scales1",
+            "w3_grouped0": "w2_codes0",
+            "w3_grouped1": "w2_scales0",
+        }
+
         def sbuf(name, shape, dtype):
-            return sb.tile(shape, dtype, name=name, align_bytes=64)
+            return sb.tile(shape, dtype, name=name, tag=shared.get(name, name), align_bytes=64)
 
 
         def load_weight(name, w, tag):
@@ -93,7 +100,7 @@ def tile_picked_ygunet_none_po_kernel(
 
         xs = sbuf("xs", [P, S], U8)
         nc.vector.tensor_copy(xs[:], xs_all[:].indirect(offs_sb[:]))
-        w1_g = [round_pair("w1", w1_raw, pair, nc.scalar.copy) for pair in range(2)]
+        w1_g = [round_pair("w1", w1_raw, 0, nc.vector.tensor_copy), round_pair("w1", w1_raw, 1, nc.scalar.copy)]
         w3_raw = load_weight("w3", w3, "stage_a")
         w1_q = [quantize_pair("w1", w1_g[0], 0)]
         halves = [slice(0, HALF), slice(HALF, S)]

@@ -30,10 +30,7 @@ def tile_picked_ygunet_none_po_kernel(
         ps = ctx.enter_context(tc.psum_pool(name="ps", bufs=1))
 
         shared = {
-            "w2_grouped0": "w1_codes1",
-            "w2_grouped1": "w1_scales1",
-            "w3_grouped0": "w2_codes0",
-            "w3_grouped1": "w2_scales0",
+            "w3_grouped0": "w1_codes1",
         }
 
         def sbuf(name, shape, dtype):
@@ -45,8 +42,9 @@ def tile_picked_ygunet_none_po_kernel(
             nc.sync.dma_start(out=raw[:], in_=w.rearrange("(p j) c -> p j c", j=PACK))
             return raw
 
-        def round_pair(name, raw, pair, copy):
-            grouped = sbuf("%s_grouped%d" % (name, pair), [P, 2, P, PACK], BF16)
+        def round_pair(name, raw, pair, copy, grouped=None):
+            if grouped is None:
+                grouped = sbuf("%s_grouped%d" % (name, pair), [P, 2, P, PACK], BF16)
             src = raw[:].rearrange("p j (m t) -> p m j t", t=PACK)[:, :, :, 2 * pair : 2 * pair + 2]
             copy(out=grouped[:].rearrange("p t m j -> p m j t"), in_=src)
             return grouped
@@ -79,18 +77,18 @@ def tile_picked_ygunet_none_po_kernel(
         nc.vector.memset(xs_all[:].bitcast(I32), 0)
         offs_sb = sbuf("offs_sb", [P, S // 16], U16)
         nc.sync.dma_start(offs_sb[:], offs)
+        w1_raw = load_weight("w1", w1, "stage_a")
         kept_sb = sbuf("kept_sb", [P, V // 16], U16)
         nc.sync.dma_start(kept_sb[:], kept)
-        w1_raw = load_weight("w1", w1, "stage_a")
         for q in range(4):
-            nc.scalar.dma_start(
+            nc.sync.dma_start(
                 out=xs_all[32 * q : 32 * q + 4, :].bitcast(I32), in_=x_scales[0, 4 * q : 4 * q + 4, :].bitcast(I32)
             )
         xw_all = sbuf("xw_all", [P, T], I32)
         nc.sync.dma_start(out=xw_all[:], in_=x_words[0].rearrange("p n t -> p (n t)").bitcast(I32))
         score_sb = sbuf("score_sb", [P, S], F32)
         nc.sync.dma_start(out=score_sb[:], in_=score)
-        w2_raw = load_weight("w2", w2, "stage_b")
+        w3_raw = load_weight("w3", w3, "stage_b")
 
         up = [sbuf("up%d" % t, [P, S], F32) for t in range(PACK)]
         for t in range(PACK):
@@ -101,7 +99,7 @@ def tile_picked_ygunet_none_po_kernel(
         xs = sbuf("xs", [P, S], U8)
         nc.vector.tensor_copy(xs[:], xs_all[:].indirect(offs_sb[:]))
         w1_g = [round_pair("w1", w1_raw, 0, nc.vector.tensor_copy), round_pair("w1", w1_raw, 1, nc.scalar.copy)]
-        w3_raw = load_weight("w3", w3, "stage_a")
+        w2_raw = load_weight("w2", w2, "stage_a")
         w1_q = [quantize_pair("w1", w1_g[0], 0)]
         halves = [slice(0, HALF), slice(HALF, S)]
         xw = sbuf("xw", [P, S], U32)
@@ -115,24 +113,26 @@ def tile_picked_ygunet_none_po_kernel(
         z = sbuf("z", [P, PACK, V], F32)
         h = [sbuf("h%d" % t, [P, S], F32) for t in range(PACK)]
 
-        def hidden(t, i):
-            h_ps = ps.tile([P, HALF], F32, name="h_ps", tag="bank%d" % (2 * t + i))
-            product(h_ps[:], w1_q, t, xw[:, halves[i]], xs[:, halves[i]])
-            nc.scalar.activation(h[t][:, halves[i]], h_ps[:], RELU)
+        def hidden(t, cols, bank):
+            h_ps = ps.tile([P, cols.stop - cols.start], F32, name="h_ps", tag="bank%d" % bank)
+            product(h_ps[:], w1_q, t, xw[:, cols], xs[:, cols])
+            nc.scalar.activation(h[t][:, cols], h_ps[:], RELU)
 
         def weigh(t):
             nc.vector.tensor_tensor(z[:, t, :], h[t][:].indirect(kept_sb[:]), score_kept[:], MULT)
 
-        hidden(0, 0)
-        hidden(1, 0)
-        hidden(0, 1)
+        whole = slice(0, S)
+        hidden(0, halves[0], 0)
+        hidden(1, halves[0], 1)
+        hidden(0, halves[1], 2)
         weigh(0)
-        hidden(1, 1)
+        hidden(1, halves[1], 3)
         weigh(1)
         for t in (2, 3):
-            hidden(t, 0)
-            hidden(t, 1)
+            hidden(t, whole, 2 + t)
             weigh(t)
+        w3_g = [round_pair("w3", w3_raw, 0, nc.scalar.copy)]
+        w3_q = [quantize_pair("w3", w3_g[0], 0)]
         w2_g = [round_pair("w2", w2_raw, pair, nc.scalar.copy) for pair in range(2)]
         z_grouped = sbuf("z_grouped", [P, V, PACK], BF16)
         z_codes = sbuf("z_codes", [P, V], U32)
@@ -172,25 +172,26 @@ def tile_picked_ygunet_none_po_kernel(
         def add(t, cols):
             nc.vector.tensor_tensor(result[:, t, cols], up[t][:, cols], y_ps[t][:, cols], ADD)
 
-        whole = slice(0, S)
+        def add_aside(t):
+            y = w2_raw[:, t, :]
+            nc.scalar.copy(y, y_ps[t][:])
+            nc.gpsimd.tensor_tensor(result[:, t, :], up[t][:], y, ADD)
+            nc.sync.dma_start(out=out_rows[:, t, :], in_=result[:, t, :])
+
         scatter(0, z_halves[0], 0)
         scatter(0, z_halves[1], 1)
-        w3_g = [round_pair("w3", w3_raw, 0, nc.scalar.copy)]
-        w3_q = [quantize_pair("w3", w3_g[0], 0)]
         skip(0)
         skip(1)
         scatter(1, slice(0, V), 2)
-        w3_g.append(round_pair("w3", w3_raw, 1, nc.scalar.copy))
-        for t in range(2):
-            add(t, whole)
-            nc.sync.dma_start(out=out_rows[:, t, :], in_=result[:, t, :])
+        add_aside(0)
+        w3_g.append(round_pair("w3", w3_raw, 1, nc.scalar.copy, w2_g[0]))
         w3_q.append(quantize_pair("w3", w3_g[1], 1))
         skip(2)
         skip(3)
         scatter(2, slice(0, V), 3)
-        add(2, whole)
-        nc.sync.dma_start(out=out_rows[:, 2, :], in_=result[:, 2, :])
+        add_aside(1)
         scatter(3, slice(0, V), 0)
+        add_aside(2)
         add(3, halves[0])
         add(3, halves[1])
         nc.sync.dma_start(out=out_rows[:, 3, :], in_=result[:, 3, :])

@@ -157,16 +157,18 @@ def tile_picked_ygunet_none_po_kernel(
         out_rows = out_0.rearrange("(p t) n -> p t n", t=PACK)
         y_ps = {}
 
+        banks = [ps.tile([P, S], F32, name="bank", tag="bank%d" % b) for b in (0, 1, 2, 3, 4, 6, 7)]
+
         def scatter(t, cols, bank):
             width = cols.stop - cols.start
-            rr_ps = ps.tile([P, width], F32, name="rr_ps", tag="bank%d" % bank)
-            product(rr_ps[:], w2_q, t, z_codes[:, cols], z_scales[:, cols])
+            rr_ps = banks[bank][:, 0:width]
+            product(rr_ps, w2_q, t, z_codes[:, cols], z_scales[:, cols])
             rr = sbuf("rr%d_%d" % (t, cols.start), [P, width], F32)
-            nc.scalar.copy(rr[:], rr_ps[:])
+            nc.scalar.copy(rr[:], rr_ps)
             nc.vector.tensor_copy(up[t][:].indirect(kept_sb[:, cols.start // 16 : cols.stop // 16]), rr[:])
 
         def skip(t):
-            y_ps[t] = ps.tile([P, S], F32, name="y_ps", tag="bank%d" % (4 + t))
+            y_ps[t] = banks[t if t < 2 else 3 + t]
             product(y_ps[t][:], w3_q, t, xw[:], xs[:])
 
         def add(t, cols):
@@ -190,7 +192,7 @@ def tile_picked_ygunet_none_po_kernel(
         skip(3)
         scatter(2, slice(0, V), 3)
         add_aside(1)
-        scatter(3, slice(0, V), 0)
+        scatter(3, slice(0, V), 4)
         add_aside(2)
         add(3, halves[0])
         add(3, halves[1])

@@ -18,7 +18,20 @@ ADD = mybir.AluOpType.add
 
 P = 128
 PACK = 4
-HALF = S // 2
+WEIGHT_COLS = PACK * P
+LIST_ROWS = 16
+QUADRANT = 32
+SCALE_ROWS = 4
+LINE = 4
+ALIGN = 64
+
+
+def halves_of(width):
+    return [slice(0, width // 2), slice(width // 2, width)]
+
+
+def list_columns(entries):
+    return slice(entries.start // LIST_ROWS, entries.stop // LIST_ROWS)
 
 
 def tile_picked_ygunet_none_po_kernel(
@@ -29,39 +42,41 @@ def tile_picked_ygunet_none_po_kernel(
         sb = ctx.enter_context(tc.tile_pool(name="sb", bufs=1))
         ps = ctx.enter_context(tc.psum_pool(name="ps", bufs=1))
 
-        shared = {
+        successor_of = {
+            "w2_raw": "w1_raw",
+            "w1_scales1": "xw_all",
             "w3_grouped0": "w1_codes1",
         }
 
         def sbuf(name, shape, dtype):
-            return sb.tile(shape, dtype, name=name, tag=shared.get(name, name), align_bytes=64)
+            return sb.tile(shape, dtype, name=name, tag=successor_of.get(name, name), align_bytes=ALIGN)
 
-
-        def load_weight(name, w, tag):
-            raw = sb.tile([P, PACK, 512], F32, name=name + "_raw", tag=tag, align_bytes=64)
+        def load_weight(name, w):
+            raw = sbuf(name + "_raw", [P, PACK, WEIGHT_COLS], F32)
             nc.sync.dma_start(out=raw[:], in_=w.rearrange("(p j) c -> p j c", j=PACK))
             return raw
 
-        def round_pair(name, raw, pair, copy, grouped=None):
-            if grouped is None:
-                grouped = sbuf("%s_grouped%d" % (name, pair), [P, 2, P, PACK], BF16)
+        def grouped_pair(name, pair):
+            return sbuf("%s_grouped%d" % (name, pair), [P, 2, P, PACK], BF16)
+
+        def round_pair(grouped, raw, pair, copy):
             src = raw[:].rearrange("p j (m t) -> p m j t", t=PACK)[:, :, :, 2 * pair : 2 * pair + 2]
-            copy(out=grouped[:].rearrange("p t m j -> p m j t"), in_=src)
+            copy(out=grouped[:].rearrange("p u m j -> p m j u"), in_=src)
             return grouped
 
         def quantize_pair(name, grouped, pair):
             codes = sbuf("%s_codes%d" % (name, pair), [P, 2 * P], U32)
             scales = sbuf("%s_scales%d" % (name, pair), [P, 2 * P], U8)
             nc.vector.quantize_mx(
-                out=codes[:].bitcast(FP8X4), scales=scales[:], in_=grouped[:].rearrange("p t m j -> p (t m j)")
+                out=codes[:].bitcast(FP8X4), scales=scales[:], in_=grouped[:].rearrange("p u m j -> p (u m j)")
             )
             return codes, scales
 
-        def product(bank, weight, t, codes, scales):
-            w_codes, w_scales = weight[t // 2]
+        def product(out, weight_pairs, t, codes, scales):
+            w_codes, w_scales = weight_pairs[t // 2]
             cols = slice((t % 2) * P, (t % 2 + 1) * P)
             nc.tensor.matmul_mx(
-                out=bank,
+                out=out,
                 lhsT=w_codes[:, cols].bitcast(FP8X4),
                 lhsT_scale=w_scales[:, cols],
                 rhs=codes.bitcast(FP8X4),
@@ -71,42 +86,49 @@ def tile_picked_ygunet_none_po_kernel(
             )
 
         def interleave(copy, dst, src):
-            copy(out=dst.rearrange("p (c i) t -> p c t i", i=4), in_=src.rearrange("p t (c i) -> p c t i", i=4))
+            copy(
+                out=dst.rearrange("p (c i) t -> p c t i", i=LINE),
+                in_=src.rearrange("p t (c i) -> p c t i", i=LINE),
+            )
+
+        def scale_rows(tile, dram, q):
+            in_sbuf = tile[QUADRANT * q : QUADRANT * q + SCALE_ROWS, :]
+            in_dram = dram[0, SCALE_ROWS * q : SCALE_ROWS * (q + 1), :]
+            return in_sbuf.bitcast(I32), in_dram.bitcast(I32)
 
         xs_all = sbuf("xs_all", [P, T], U8)
         nc.vector.memset(xs_all[:].bitcast(I32), 0)
-        offs_sb = sbuf("offs_sb", [P, S // 16], U16)
+        w1_raw = load_weight("w1", w1)
+        offs_sb = sbuf("offs_sb", [P, S // LIST_ROWS], U16)
         nc.sync.dma_start(offs_sb[:], offs)
-        w1_raw = load_weight("w1", w1, "stage_a")
-        kept_sb = sbuf("kept_sb", [P, V // 16], U16)
+        kept_sb = sbuf("kept_sb", [P, V // LIST_ROWS], U16)
         nc.sync.dma_start(kept_sb[:], kept)
-        for q in range(4):
-            nc.sync.dma_start(
-                out=xs_all[32 * q : 32 * q + 4, :].bitcast(I32), in_=x_scales[0, 4 * q : 4 * q + 4, :].bitcast(I32)
-            )
+        for q in range(P // QUADRANT):
+            in_sbuf, in_dram = scale_rows(xs_all, x_scales, q)
+            nc.sync.dma_start(out=in_sbuf, in_=in_dram)
         xw_all = sbuf("xw_all", [P, T], I32)
-        nc.sync.dma_start(out=xw_all[:], in_=x_words[0].rearrange("p n t -> p (n t)").bitcast(I32))
+        nc.sync.dma_start(out=xw_all[:], in_=x_words[0].rearrange("p n j -> p (n j)").bitcast(I32))
         score_sb = sbuf("score_sb", [P, S], F32)
         nc.sync.dma_start(out=score_sb[:], in_=score)
-        w3_raw = load_weight("w3", w3, "stage_b")
+        w3_raw = load_weight("w3", w3)
 
         up = [sbuf("up%d" % t, [P, S], F32) for t in range(PACK)]
         for t in range(PACK):
             nc.vector.memset(up[t][:], 0.0)
-        warm = sbuf("warm", [P, 1], F32)
-        nc.scalar.activation(warm[:], up[0][:, 0:1], RELU)
 
         xs = sbuf("xs", [P, S], U8)
         nc.vector.tensor_copy(xs[:], xs_all[:].indirect(offs_sb[:]))
-        w1_g = [round_pair("w1", w1_raw, 0, nc.vector.tensor_copy), round_pair("w1", w1_raw, 1, nc.scalar.copy)]
-        w2_raw = load_weight("w2", w2, "stage_a")
-        w1_q = [quantize_pair("w1", w1_g[0], 0)]
-        halves = [slice(0, HALF), slice(HALF, S)]
+        w1_grouped = [
+            round_pair(grouped_pair("w1", 0), w1_raw, 0, nc.vector.tensor_copy),
+            round_pair(grouped_pair("w1", 1), w1_raw, 1, nc.scalar.copy),
+        ]
+        w2_raw = load_weight("w2", w2)
+        w1_pairs = [quantize_pair("w1", w1_grouped[0], 0)]
+        node_halves = halves_of(S)
         xw = sbuf("xw", [P, S], U32)
-        for i in range(2):
-            entries = offs_sb[:, i * (HALF // 16) : (i + 1) * (HALF // 16)]
-            nc.vector.tensor_copy(xw[:, halves[i]], xw_all[:].bitcast(U32).indirect(entries))
-        w1_q.append(quantize_pair("w1", w1_g[1], 1))
+        for cols in node_halves:
+            nc.vector.tensor_copy(xw[:, cols], xw_all[:].bitcast(U32).indirect(offs_sb[:, list_columns(cols)]))
+        w1_pairs.append(quantize_pair("w1", w1_grouped[1], 1))
         score_kept = sbuf("score_kept", [P, V], F32)
         nc.vector.tensor_copy(score_kept[:], score_sb[:].indirect(kept_sb[:]))
 
@@ -115,104 +137,102 @@ def tile_picked_ygunet_none_po_kernel(
 
         def hidden(t, cols, bank):
             h_ps = ps.tile([P, cols.stop - cols.start], F32, name="h_ps", tag="bank%d" % bank)
-            product(h_ps[:], w1_q, t, xw[:, cols], xs[:, cols])
+            product(h_ps[:], w1_pairs, t, xw[:, cols], xs[:, cols])
             nc.scalar.activation(h[t][:, cols], h_ps[:], RELU)
 
         def weigh(t):
             nc.vector.tensor_tensor(z[:, t, :], h[t][:].indirect(kept_sb[:]), score_kept[:], MULT)
 
-        whole = slice(0, S)
-        hidden(0, halves[0], 0)
-        hidden(1, halves[0], 1)
-        hidden(0, halves[1], 2)
+        hidden(0, node_halves[0], bank=0)
+        hidden(1, node_halves[0], bank=1)
+        hidden(0, node_halves[1], bank=2)
         weigh(0)
-        hidden(1, halves[1], 3)
+        hidden(1, node_halves[1], bank=3)
         weigh(1)
-        for t in (2, 3):
-            hidden(t, whole, 2 + t)
-            weigh(t)
-        w3_g = [round_pair("w3", w3_raw, 0, nc.scalar.copy)]
-        w3_q = [quantize_pair("w3", w3_g[0], 0)]
-        w2_g = [round_pair("w2", w2_raw, pair, nc.scalar.copy) for pair in range(2)]
+        hidden(2, slice(0, S), bank=4)
+        weigh(2)
+        hidden(3, slice(0, S), bank=5)
+        weigh(3)
+
+        w3_pairs = [quantize_pair("w3", round_pair(grouped_pair("w3", 0), w3_raw, 0, nc.scalar.copy), 0)]
+        w2_grouped = [round_pair(grouped_pair("w2", pair), w2_raw, pair, nc.scalar.copy) for pair in range(2)]
         z_grouped = sbuf("z_grouped", [P, V, PACK], BF16)
         z_codes = sbuf("z_codes", [P, V], U32)
         z_scales = sbuf("z_scales", [P, V], U8)
-        z_halves = [slice(0, V // 2), slice(V // 2, V)]
+        kept_halves = halves_of(V)
 
-        def quantize_z(cols):
+        def quantize_z(entries):
             nc.vector.quantize_mx(
-                out=z_codes[:, cols].bitcast(FP8X4),
-                scales=z_scales[:, cols],
-                in_=z_grouped[:, cols, :].rearrange("p v t -> p (v t)"),
+                out=z_codes[:, entries].bitcast(FP8X4),
+                scales=z_scales[:, entries],
+                in_=z_grouped[:, entries, :].rearrange("p v t -> p (v t)"),
             )
 
-        interleave(nc.vector.tensor_copy, z_grouped[:, z_halves[0], :], z[:, :, z_halves[0]])
-        w2_q = [quantize_pair("w2", w2_g[0], 0)]
-        quantize_z(z_halves[0])
-        interleave(nc.vector.tensor_copy, z_grouped[:, z_halves[1], :], z[:, :, z_halves[1]])
-        quantize_z(z_halves[1])
-        w2_q.append(quantize_pair("w2", w2_g[1], 1))
+        interleave(nc.vector.tensor_copy, z_grouped[:, kept_halves[0], :], z[:, :, kept_halves[0]])
+        w2_pairs = [quantize_pair("w2", w2_grouped[0], 0)]
+        quantize_z(kept_halves[0])
+        interleave(nc.vector.tensor_copy, z_grouped[:, kept_halves[1], :], z[:, :, kept_halves[1]])
+        quantize_z(kept_halves[1])
+        w2_pairs.append(quantize_pair("w2", w2_grouped[1], 1))
 
         result = sbuf("result", [P, PACK, S], F32)
         out_rows = out_0.rearrange("(p t) n -> p t n", t=PACK)
-        y_ps = {}
+        banks = {b: ps.tile([P, S], F32, name="bank", tag="bank%d" % b) for b in (0, 1, 2, 3, 4, 6, 7)}
+        y_ps = [banks[0], banks[1], banks[6], banks[7]]
 
-        banks = [ps.tile([P, S], F32, name="bank", tag="bank%d" % b) for b in (0, 1, 2, 3, 4, 6, 7)]
-
-        def scatter(t, cols, bank):
-            width = cols.stop - cols.start
+        def put_back(t, entries, bank):
+            width = entries.stop - entries.start
             rr_ps = banks[bank][:, 0:width]
-            product(rr_ps, w2_q, t, z_codes[:, cols], z_scales[:, cols])
-            rr = sbuf("rr%d_%d" % (t, cols.start), [P, width], F32)
+            product(rr_ps, w2_pairs, t, z_codes[:, entries], z_scales[:, entries])
+            rr = sbuf("rr%d_%d" % (t, entries.start), [P, width], F32)
             nc.scalar.copy(rr[:], rr_ps)
-            nc.vector.tensor_copy(up[t][:].indirect(kept_sb[:, cols.start // 16 : cols.stop // 16]), rr[:])
+            nc.vector.tensor_copy(up[t][:].indirect(kept_sb[:, list_columns(entries)]), rr[:])
 
         def skip(t):
-            y_ps[t] = banks[t if t < 2 else 3 + t]
-            product(y_ps[t][:], w3_q, t, xw[:], xs[:])
+            product(y_ps[t][:], w3_pairs, t, xw[:], xs[:])
 
-        def add(t, cols):
-            nc.vector.tensor_tensor(result[:, t, cols], up[t][:, cols], y_ps[t][:, cols], ADD)
+        def store_quarter(t):
+            nc.sync.dma_start(out=out_rows[:, t, :], in_=result[:, t, :])
 
-        def add_aside(t):
+        def add_on_gpsimd(t):
             y = w2_raw[:, t, :]
             nc.scalar.copy(y, y_ps[t][:])
             nc.gpsimd.tensor_tensor(result[:, t, :], up[t][:], y, ADD)
-            nc.sync.dma_start(out=out_rows[:, t, :], in_=result[:, t, :])
+            store_quarter(t)
 
-        scatter(0, z_halves[0], 0)
-        scatter(0, z_halves[1], 1)
+        all_kept = slice(0, V)
+        put_back(0, kept_halves[0], bank=0)
+        put_back(0, kept_halves[1], bank=1)
         skip(0)
         skip(1)
-        scatter(1, slice(0, V), 2)
-        add_aside(0)
-        w3_g.append(round_pair("w3", w3_raw, 1, nc.scalar.copy, w2_g[0]))
-        w3_q.append(quantize_pair("w3", w3_g[1], 1))
+        put_back(1, all_kept, bank=2)
+        add_on_gpsimd(0)
+        w3_pairs.append(quantize_pair("w3", round_pair(w2_grouped[0], w3_raw, 1, nc.scalar.copy), 1))
         skip(2)
         skip(3)
-        scatter(2, slice(0, V), 3)
-        add_aside(1)
-        scatter(3, slice(0, V), 4)
-        add_aside(2)
-        add(3, halves[0])
-        add(3, halves[1])
-        nc.sync.dma_start(out=out_rows[:, 3, :], in_=result[:, 3, :])
+        put_back(2, all_kept, bank=3)
+        add_on_gpsimd(1)
+        put_back(3, all_kept, bank=4)
+        add_on_gpsimd(2)
+        last = PACK - 1
+        for cols in node_halves:
+            nc.vector.tensor_tensor(result[:, last, cols], up[last][:, cols], y_ps[last][:, cols], ADD)
+        store_quarter(last)
 
         o_scales = sbuf("o_scales", [P, S], U8)
-        words = out_1[0].rearrange("p n t -> p (n t)").bitcast(I32)
-        o_grouped = [sbuf("o_grouped%d" % i, [P, HALF, PACK], BF16) for i in range(2)]
-        interleave(nc.scalar.copy, o_grouped[0][:], result[:, :, halves[0]])
-        interleave(nc.vector.tensor_copy, o_grouped[1][:], result[:, :, halves[1]])
-        for i in (1, 0):
-            o_codes = sbuf("o_codes%d" % i, [P, HALF], I32)
+        out_words = out_1[0].rearrange("p n j -> p (n j)").bitcast(I32)
+        o_grouped = [sbuf("o_grouped%d" % half, [P, S // 2, PACK], BF16) for half in range(2)]
+        interleave(nc.scalar.copy, o_grouped[0][:], result[:, :, node_halves[0]])
+        interleave(nc.vector.tensor_copy, o_grouped[1][:], result[:, :, node_halves[1]])
+        for half in (1, 0):
+            o_codes = sbuf("o_codes%d" % half, [P, S // 2], I32)
             nc.vector.quantize_mx(
                 out=o_codes[:].bitcast(FP8X4),
-                scales=o_scales[:, halves[i]],
-                in_=o_grouped[i][:].rearrange("p n t -> p (n t)"),
+                scales=o_scales[:, node_halves[half]],
+                in_=o_grouped[half][:].rearrange("p n t -> p (n t)"),
             )
-            nc.sync.dma_start(out=words[:, halves[i]], in_=o_codes[:])
-        for q in range(4):
+            nc.sync.dma_start(out=out_words[:, node_halves[half]], in_=o_codes[:])
+        for q in range(P // QUADRANT):
             queue = nc.scalar if q % 2 == 0 else nc.sync
-            queue.dma_start(
-                out=out_2[0, 4 * q : 4 * q + 4, :].bitcast(I32), in_=o_scales[32 * q : 32 * q + 4, :].bitcast(I32)
-            )
+            in_sbuf, in_dram = scale_rows(o_scales, out_2, q)
+            queue.dma_start(out=in_dram, in_=in_sbuf)

@@ -41,11 +41,10 @@ def tile_picked_ygunet_none_po_kernel(
     with ExitStack() as ctx:
         sb = ctx.enter_context(tc.tile_pool(name="sb", bufs=1))
         ps = ctx.enter_context(tc.psum_pool(name="ps", bufs=1))
+        shared = ctx.enter_context(tc.tile_pool(name="shared", bufs=1))
 
         successor_of = {
-            "w2_raw": "w1_raw",
             "w1_scales1": "xw_all",
-            "w3_grouped0": "w1_codes1",
         }
 
         def sbuf(name, shape, dtype):
@@ -57,18 +56,20 @@ def tile_picked_ygunet_none_po_kernel(
             return raw
 
         def grouped_pair(name, pair):
-            return sbuf("%s_grouped%d" % (name, pair), [P, 2, P, PACK], BF16)
+            return sbuf("%s_grouped%d" % (name, pair), [P, 2, P, PACK], BF16)[:]
 
-        def round_pair(grouped, raw, pair, copy):
+        def round_pair(grouped, raw, pair, copy, pieces=(slice(0, P),)):
             src = raw[:].rearrange("p j (m t) -> p m j t", t=PACK)[:, :, :, 2 * pair : 2 * pair + 2]
-            copy(out=grouped[:].rearrange("p u m j -> p m j u"), in_=src)
+            dst = grouped.rearrange("p u m j -> p m j u")
+            for places in pieces:
+                copy(out=dst[:, places], in_=src[:, places])
             return grouped
 
         def quantize_pair(name, grouped, pair):
             codes = sbuf("%s_codes%d" % (name, pair), [P, 2 * P], U32)
             scales = sbuf("%s_scales%d" % (name, pair), [P, 2 * P], U8)
             nc.vector.quantize_mx(
-                out=codes[:].bitcast(FP8X4), scales=scales[:], in_=grouped[:].rearrange("p u m j -> p (u m j)")
+                out=codes[:].bitcast(FP8X4), scales=scales[:], in_=grouped.rearrange("p u m j -> p (u m j)")
             )
             return codes, scales
 
@@ -110,6 +111,7 @@ def tile_picked_ygunet_none_po_kernel(
         nc.sync.dma_start(out=xw_all[:], in_=x_words[0].rearrange("p n j -> p (n j)").bitcast(I32))
         score_sb = sbuf("score_sb", [P, S], F32)
         nc.sync.dma_start(out=score_sb[:], in_=score)
+        w2_raw = load_weight("w2", w2)
         w3_raw = load_weight("w3", w3)
 
         up = [sbuf("up%d" % t, [P, S], F32) for t in range(PACK)]
@@ -122,7 +124,6 @@ def tile_picked_ygunet_none_po_kernel(
             round_pair(grouped_pair("w1", 0), w1_raw, 0, nc.vector.tensor_copy),
             round_pair(grouped_pair("w1", 1), w1_raw, 1, nc.scalar.copy),
         ]
-        w2_raw = load_weight("w2", w2)
         w1_pairs = [quantize_pair("w1", w1_grouped[0], 0)]
         node_halves = halves_of(S)
         xw = sbuf("xw", [P, S], U32)
@@ -140,53 +141,71 @@ def tile_picked_ygunet_none_po_kernel(
             product(h_ps[:], w1_pairs, t, xw[:, cols], xs[:, cols])
             nc.scalar.activation(h[t][:, cols], h_ps[:], RELU)
 
-        def weigh(t):
-            nc.vector.tensor_tensor(z[:, t, :], h[t][:].indirect(kept_sb[:]), score_kept[:], MULT)
+        kept_halves = halves_of(V)
+        all_kept = slice(0, V)
+
+        def weigh(t, entries):
+            window = h[t][:].indirect(kept_sb[:, list_columns(entries)])
+            nc.vector.tensor_tensor(z[:, t, entries], window, score_kept[:, entries], MULT)
 
         hidden(0, node_halves[0], bank=0)
         hidden(1, node_halves[0], bank=1)
         hidden(0, node_halves[1], bank=2)
-        weigh(0)
+        weigh(0, all_kept)
         hidden(1, node_halves[1], bank=3)
-        weigh(1)
+        weigh(1, all_kept)
         hidden(2, slice(0, S), bank=4)
-        weigh(2)
+        weigh(2, all_kept)
         hidden(3, slice(0, S), bank=5)
-        weigh(3)
+        for entries in kept_halves:
+            weigh(3, entries)
 
-        w3_pairs = [quantize_pair("w3", round_pair(grouped_pair("w3", 0), w3_raw, 0, nc.scalar.copy), 0)]
-        w2_grouped = [round_pair(grouped_pair("w2", pair), w2_raw, pair, nc.scalar.copy) for pair in range(2)]
-        z_grouped = sbuf("z_grouped", [P, V, PACK], BF16)
+        half = V // 2
+        w2_grouped = [
+            shared.tile([P, 2, P, PACK], BF16, name="w2_grouped0", offset=0, align_bytes=ALIGN)[:],
+            grouped_pair("w2", 1),
+        ]
+        for pair in range(2):
+            round_pair(w2_grouped[pair], w2_raw, pair, nc.scalar.copy, halves_of(P))
+        z_grouped = [
+            sbuf("z_grouped0", [P, half, PACK], BF16),
+            shared.tile([P, half, PACK], BF16, name="z_grouped1", offset=1024, align_bytes=ALIGN),
+        ]
         z_codes = sbuf("z_codes", [P, V], U32)
-        z_scales = sbuf("z_scales", [P, V], U8)
-        kept_halves = halves_of(V)
+        z_scales = [
+            shared.tile([P, half], U8, name="z_scales0", offset=0, align_bytes=ALIGN),
+            sbuf("z_scales1", [P, half], U8),
+        ]
 
-        def quantize_z(entries):
+        def round_z(i):
+            interleave(nc.vector.tensor_copy, z_grouped[i][:], z[:, :, kept_halves[i]])
+
+        def quantize_z(i):
             nc.vector.quantize_mx(
-                out=z_codes[:, entries].bitcast(FP8X4),
-                scales=z_scales[:, entries],
-                in_=z_grouped[:, entries, :].rearrange("p v t -> p (v t)"),
+                out=z_codes[:, kept_halves[i]].bitcast(FP8X4),
+                scales=z_scales[i][:],
+                in_=z_grouped[i][:].rearrange("p v t -> p (v t)"),
             )
 
-        interleave(nc.vector.tensor_copy, z_grouped[:, kept_halves[0], :], z[:, :, kept_halves[0]])
+        round_z(0)
         w2_pairs = [quantize_pair("w2", w2_grouped[0], 0)]
-        quantize_z(kept_halves[0])
-        interleave(nc.vector.tensor_copy, z_grouped[:, kept_halves[1], :], z[:, :, kept_halves[1]])
-        quantize_z(kept_halves[1])
+        quantize_z(0)
+        round_z(1)
         w2_pairs.append(quantize_pair("w2", w2_grouped[1], 1))
+        quantize_z(1)
 
         result = sbuf("result", [P, PACK, S], F32)
         out_rows = out_0.rearrange("(p t) n -> p t n", t=PACK)
-        banks = {b: ps.tile([P, S], F32, name="bank", tag="bank%d" % b) for b in (0, 1, 2, 3, 4, 6, 7)}
-        y_ps = [banks[0], banks[1], banks[6], banks[7]]
+        banks = {b: ps.tile([P, S], F32, name="bank", tag="bank%d" % b) for b in range(8)}
+        y_ps = [banks[6], banks[7], banks[0], banks[1]]
 
-        def put_back(t, entries, bank):
-            width = entries.stop - entries.start
-            rr_ps = banks[bank][:, 0:width]
-            product(rr_ps, w2_pairs, t, z_codes[:, entries], z_scales[:, entries])
-            rr = sbuf("rr%d_%d" % (t, entries.start), [P, width], F32)
-            nc.scalar.copy(rr[:], rr_ps)
-            nc.vector.tensor_copy(up[t][:].indirect(kept_sb[:, list_columns(entries)]), rr[:])
+        def put_back(t, halves, bank, staged):
+            entries = slice(kept_halves[halves[0]].start, kept_halves[halves[-1]].stop)
+            for i in halves:
+                cols = slice(kept_halves[i].start - entries.start, kept_halves[i].stop - entries.start)
+                product(banks[bank][:, cols], w2_pairs, t, z_codes[:, kept_halves[i]], z_scales[i][:])
+            nc.scalar.copy(staged, banks[bank][:, 0 : entries.stop - entries.start])
+            nc.vector.tensor_copy(up[t][:].indirect(kept_sb[:, list_columns(entries)]), staged)
 
         def skip(t):
             product(y_ps[t][:], w3_pairs, t, xw[:], xs[:])
@@ -200,20 +219,24 @@ def tile_picked_ygunet_none_po_kernel(
             nc.gpsimd.tensor_tensor(result[:, t, :], up[t][:], y, ADD)
             store_quarter(t)
 
-        all_kept = slice(0, V)
-        put_back(0, kept_halves[0], bank=0)
-        put_back(0, kept_halves[1], bank=1)
+        rr = sbuf("rr", [P, 3, half], F32)
+        put_back(0, (0,), 0, rr[:, 0, :])
+        put_back(1, (0,), 1, rr[:, 1, :])
+        put_back(0, (1,), 2, rr[:, 2, :])
+        w3_pairs = []
+        for pair in range(2):
+            grouped = round_pair(grouped_pair("w3", pair), w3_raw, pair, nc.scalar.copy, halves_of(P))
+            w3_pairs.append(quantize_pair("w3", grouped, pair))
+        put_back(1, (1,), 3, w3_raw[:, 0, 0:half])
+        put_back(2, (0, 1), 4, w3_raw[:, 1, 0:V])
         skip(0)
-        skip(1)
-        put_back(1, all_kept, bank=2)
         add_on_gpsimd(0)
-        w3_pairs.append(quantize_pair("w3", round_pair(w2_grouped[0], w3_raw, 1, nc.scalar.copy), 1))
-        skip(2)
-        skip(3)
-        put_back(2, all_kept, bank=3)
+        skip(1)
         add_on_gpsimd(1)
-        put_back(3, all_kept, bank=4)
+        put_back(3, (0, 1), 5, w3_raw[:, 2, 0:V])
+        skip(2)
         add_on_gpsimd(2)
+        skip(3)
         last = PACK - 1
         for cols in node_halves:
             nc.vector.tensor_tensor(result[:, last, cols], up[last][:, cols], y_ps[last][:, cols], ADD)
@@ -221,7 +244,7 @@ def tile_picked_ygunet_none_po_kernel(
 
         o_scales = sbuf("o_scales", [P, S], U8)
         out_words = out_1[0].rearrange("p n j -> p (n j)").bitcast(I32)
-        o_grouped = [sbuf("o_grouped%d" % half, [P, S // 2, PACK], BF16) for half in range(2)]
+        o_grouped = [sbuf("o_grouped%d" % i, [P, S // 2, PACK], BF16) for i in range(2)]
         interleave(nc.scalar.copy, o_grouped[0][:], result[:, :, node_halves[0]])
         interleave(nc.vector.tensor_copy, o_grouped[1][:], result[:, :, node_halves[1]])
         for half in (1, 0):

@@ -23,6 +23,7 @@ LIST_ROWS = 16
 QUADRANT = 32
 SCALE_ROWS = 4
 LINE = 4
+SCALAR_COLS = 128
 ALIGN = 64
 
 
@@ -93,8 +94,8 @@ def tile_picked_ygunet_none_po_kernel(
             )
 
         def scale_rows(tile, dram, q):
-            in_sbuf = tile[QUADRANT * q : QUADRANT * q + SCALE_ROWS, :]
-            in_dram = dram[0, SCALE_ROWS * q : SCALE_ROWS * (q + 1), :]
+            in_sbuf = tile[q:P:QUADRANT, :]
+            in_dram = dram[0, q : SCALE_ROWS * (P // QUADRANT) : SCALE_ROWS, :]
             return in_sbuf.bitcast(I32), in_dram.bitcast(I32)
 
         xs_all = sbuf("xs_all", [P, T], U8)
@@ -166,7 +167,7 @@ def tile_picked_ygunet_none_po_kernel(
             grouped_pair("w2", 1),
         ]
         for pair in range(2):
-            round_pair(w2_grouped[pair], w2_raw, pair, nc.scalar.copy, halves_of(P))
+            round_pair(w2_grouped[pair], w2_raw, pair, nc.scalar.copy)
         z_grouped = [
             sbuf("z_grouped0", [P, half, PACK], BF16),
             shared.tile([P, half, PACK], BF16, name="z_grouped1", offset=1024, align_bytes=ALIGN),
@@ -237,24 +238,34 @@ def tile_picked_ygunet_none_po_kernel(
         skip(2)
         add_on_gpsimd(2)
         skip(3)
+        o_scales = sbuf("o_scales", [P, S], U8)
+        out_words = out_1[0].rearrange("p n j -> p (n j)").bitcast(I32)
+        o_grouped = [sbuf("o_grouped%d" % i, [P, S // 2, PACK], BF16) for i in range(2)]
+
+        def interleave_pair(copy, i, cols, pair):
+            quarters = slice(2 * pair, 2 * pair + 2)
+            lo = node_halves[i].start
+            interleave(
+                copy, o_grouped[i][:, cols, quarters], result[:, quarters, lo + cols.start : lo + cols.stop]
+            )
+
+        for i in (1, 0):
+            interleave_pair(nc.scalar.copy, i, slice(0, S // 2), 0)
         last = PACK - 1
         for cols in node_halves:
             nc.vector.tensor_tensor(result[:, last, cols], up[last][:, cols], y_ps[last][:, cols], ADD)
         store_quarter(last)
-
-        o_scales = sbuf("o_scales", [P, S], U8)
-        out_words = out_1[0].rearrange("p n j -> p (n j)").bitcast(I32)
-        o_grouped = [sbuf("o_grouped%d" % i, [P, S // 2, PACK], BF16) for i in range(2)]
-        interleave(nc.scalar.copy, o_grouped[0][:], result[:, :, node_halves[0]])
-        interleave(nc.vector.tensor_copy, o_grouped[1][:], result[:, :, node_halves[1]])
-        for half in (1, 0):
-            o_codes = sbuf("o_codes%d" % half, [P, S // 2], I32)
+        interleave_pair(nc.scalar.copy, 0, slice(0, SCALAR_COLS), 1)
+        interleave_pair(nc.vector.tensor_copy, 0, slice(SCALAR_COLS, S // 2), 1)
+        interleave_pair(nc.vector.tensor_copy, 1, slice(0, S // 2), 1)
+        for i in (0, 1):
+            o_codes = sbuf("o_codes%d" % i, [P, S // 2], I32)
             nc.vector.quantize_mx(
                 out=o_codes[:].bitcast(FP8X4),
-                scales=o_scales[:, node_halves[half]],
-                in_=o_grouped[half][:].rearrange("p n t -> p (n t)"),
+                scales=o_scales[:, node_halves[i]],
+                in_=o_grouped[i][:].rearrange("p n t -> p (n t)"),
             )
-            nc.sync.dma_start(out=out_words[:, node_halves[half]], in_=o_codes[:])
+            nc.sync.dma_start(out=out_words[:, node_halves[i]], in_=o_codes[:])
         for q in range(P // QUADRANT):
             queue = nc.scalar if q % 2 == 0 else nc.sync
             in_sbuf, in_dram = scale_rows(o_scales, out_2, q)

@@ -18,7 +18,6 @@ ADD = mybir.AluOpType.add
 
 P = 128
 PACK = 4
-WEIGHT_COLS = PACK * P
 LIST_ROWS = 16
 QUADRANT = 32
 SCALE_ROWS = 4
@@ -27,12 +26,12 @@ SCALAR_COLS = 128
 ALIGN = 64
 
 
-def halves_of(width):
-    return [slice(0, width // 2), slice(width // 2, width)]
-
-
 def list_columns(entries):
     return slice(entries.start // LIST_ROWS, entries.stop // LIST_ROWS)
+
+
+def width(cols):
+    return cols.stop - cols.start
 
 
 def tile_picked_ygunet_none_po_kernel(
@@ -44,43 +43,36 @@ def tile_picked_ygunet_none_po_kernel(
         ps = ctx.enter_context(tc.psum_pool(name="ps", bufs=1))
         shared = ctx.enter_context(tc.tile_pool(name="shared", bufs=1))
 
-        successor_of = {
-            "w1_scales1": "xw_all",
-        }
-
         def sbuf(name, shape, dtype):
-            return sb.tile(shape, dtype, name=name, tag=successor_of.get(name, name), align_bytes=ALIGN)
+            return sb.tile(shape, dtype, name=name, tag=name, align_bytes=ALIGN)
 
-        def load_weight(name, w):
-            raw = sbuf(name + "_raw", [P, PACK, WEIGHT_COLS], F32)
-            nc.sync.dma_start(out=raw[:], in_=w.rearrange("(p j) c -> p j c", j=PACK))
+        def placed(name, shape, dtype, offset):
+            return shared.tile(shape, dtype, name=name, offset=offset, align_bytes=ALIGN)
+
+        def bank(b, name):
+            return ps.tile([P, S], F32, name=name, tag="bank%d" % b)
+
+        def load_weight(name, w, cols):
+            raw = sbuf(name, [P, PACK, width(cols)], F32)
+            nc.sync.dma_start(out=raw[:], in_=w[:, cols].rearrange("(p j) c -> p j c", j=PACK))
             return raw
 
-        def grouped_pair(name, pair):
-            return sbuf("%s_grouped%d" % (name, pair), [P, 2, P, PACK], BF16)[:]
+        def round_quarters(copy, grouped, raw, quarters, places):
+            src = raw[:].rearrange("p j (m t) -> p m j t", t=PACK)[:, places, :, quarters]
+            copy(out=grouped[:].rearrange("p u m j -> p m j u")[:, places], in_=src)
 
-        def round_pair(grouped, raw, pair, copy, pieces=(slice(0, P),)):
-            src = raw[:].rearrange("p j (m t) -> p m j t", t=PACK)[:, :, :, 2 * pair : 2 * pair + 2]
-            dst = grouped.rearrange("p u m j -> p m j u")
-            for places in pieces:
-                copy(out=dst[:, places], in_=src[:, places])
-            return grouped
+        def quantize(codes, scales, grouped):
+            nc.vector.quantize_mx(out=codes.bitcast(FP8X4), scales=scales, in_=grouped)
 
-        def quantize_pair(name, grouped, pair):
-            codes = sbuf("%s_codes%d" % (name, pair), [P, 2 * P], U32)
-            scales = sbuf("%s_scales%d" % (name, pair), [P, 2 * P], U8)
-            nc.vector.quantize_mx(
-                out=codes[:].bitcast(FP8X4), scales=scales[:], in_=grouped.rearrange("p u m j -> p (u m j)")
-            )
-            return codes, scales
+        def weight_tiles(name):
+            return sbuf(name + "_codes", [P, PACK * P], U32), sbuf(name + "_scales", [P, PACK * P], U8)
 
-        def product(out, weight_pairs, t, codes, scales):
-            w_codes, w_scales = weight_pairs[t // 2]
-            cols = slice((t % 2) * P, (t % 2 + 1) * P)
+        def product(out, weight, t, codes, scales):
+            cols = slice(t * P, (t + 1) * P)
             nc.tensor.matmul_mx(
                 out=out,
-                lhsT=w_codes[:, cols].bitcast(FP8X4),
-                lhsT_scale=w_scales[:, cols],
+                lhsT=weight[0][:, cols].bitcast(FP8X4),
+                lhsT_scale=weight[1][:, cols],
                 rhs=codes.bitcast(FP8X4),
                 rhs_scale=scales,
                 start=True,
@@ -98,173 +90,165 @@ def tile_picked_ygunet_none_po_kernel(
             in_dram = dram[0, q : SCALE_ROWS * (P // QUADRANT) : SCALE_ROWS, :]
             return in_sbuf.bitcast(I32), in_dram.bitcast(I32)
 
+        pairs = [slice(0, 2), slice(2, 4)]
+        node_halves = [slice(0, S // 2), slice(S // 2, S)]
+        place_halves = [slice(0, P // 2), slice(P // 2, P)]
+        all_places = slice(0, P)
+
+        col_halves = [slice(0, H // 2), slice(H // 2, H)]
+        kept_halves = [slice(0, V // 2), slice(V // 2, V)]
+        half = V // 2
+
+        def round_half(copy, grouped, raw, i, h):
+            src = raw[h][:].rearrange("p j (m t) -> p m j t", t=PACK)[:, :, :, pairs[i]]
+            copy(out=grouped[i][:].rearrange("p u m j -> p m j u")[:, place_halves[h]], in_=src)
+
+        def quantize_pair(weight, grouped, i):
+            cols = slice(2 * P * i, 2 * P * (i + 1))
+            quantize(weight[0][:, cols], weight[1][:, cols], grouped[:].rearrange("p u m j -> p (u m j)"))
+
         xs_all = sbuf("xs_all", [P, T], U8)
         nc.vector.memset(xs_all[:].bitcast(I32), 0)
-        w1_raw = load_weight("w1", w1)
+        xw_all = sbuf("xw_all", [P, T], I32)
+        nc.sync.dma_start(out=xw_all[:], in_=x_words[0].rearrange("p n j -> p (n j)").bitcast(I32))
         offs_sb = sbuf("offs_sb", [P, S // LIST_ROWS], U16)
         nc.sync.dma_start(offs_sb[:], offs)
-        kept_sb = sbuf("kept_sb", [P, V // LIST_ROWS], U16)
-        nc.sync.dma_start(kept_sb[:], kept)
+        w1_raw = [load_weight("w1_raw0", w1, col_halves[0])]
         for q in range(P // QUADRANT):
             in_sbuf, in_dram = scale_rows(xs_all, x_scales, q)
             nc.sync.dma_start(out=in_sbuf, in_=in_dram)
-        xw_all = sbuf("xw_all", [P, T], I32)
-        nc.sync.dma_start(out=xw_all[:], in_=x_words[0].rearrange("p n j -> p (n j)").bitcast(I32))
+        w1_raw.append(load_weight("w1_raw1", w1, col_halves[1]))
+        kept_sb = sbuf("kept_sb", [P, V // LIST_ROWS], U16)
+        nc.sync.dma_start(kept_sb[:], kept)
         score_sb = sbuf("score_sb", [P, S], F32)
         nc.sync.dma_start(out=score_sb[:], in_=score)
-        w2_raw = load_weight("w2", w2)
-        w3_raw = load_weight("w3", w3)
-
+        w2_raw = load_weight("w2_raw", w2, slice(0, N))
+        w3_raw = load_weight("w3_raw", w3, slice(0, N))
         up = [sbuf("up%d" % t, [P, S], F32) for t in range(PACK)]
         for t in range(PACK):
             nc.vector.memset(up[t][:], 0.0)
 
+        xw = sbuf("xw", [P, S], U32)
+        nc.vector.tensor_copy(xw[:], xw_all[:].bitcast(U32).indirect(offs_sb[:]))
         xs = sbuf("xs", [P, S], U8)
         nc.vector.tensor_copy(xs[:], xs_all[:].indirect(offs_sb[:]))
-        w1_grouped = [
-            round_pair(grouped_pair("w1", 0), w1_raw, 0, nc.vector.tensor_copy),
-            round_pair(grouped_pair("w1", 1), w1_raw, 1, nc.scalar.copy),
-        ]
-        w1_pairs = [quantize_pair("w1", w1_grouped[0], 0)]
-        node_halves = halves_of(S)
-        xw = sbuf("xw", [P, S], U32)
-        for cols in node_halves:
-            nc.vector.tensor_copy(xw[:, cols], xw_all[:].bitcast(U32).indirect(offs_sb[:, list_columns(cols)]))
-        w1_pairs.append(quantize_pair("w1", w1_grouped[1], 1))
+
+        w1_q = weight_tiles("w1")
+        w1_grouped = [sbuf("w1_grouped%d" % i, [P, 2, P, PACK], BF16) for i in range(2)]
+        for i in range(2):
+            round_half(nc.scalar.copy, w1_grouped, w1_raw, i, 0)
+        src = w1_raw[1][:].rearrange("p j (m t) -> p m j t", t=PACK)[:, :, :, pairs[0]]
+        dst = w1_grouped[0][:].rearrange("p u m j -> p m j u")[:, place_halves[1]]
+        nc.vector.tensor_copy(out=dst[:, 0:48], in_=src[:, 0:48])
+        nc.scalar.copy(out=dst[:, 48:64], in_=src[:, 48:64])
+        round_half(nc.scalar.copy, w1_grouped, w1_raw, 1, 1)
+        for t in range(2):
+            cols = slice(t * P, (t + 1) * P)
+            quantize(w1_q[0][:, cols], w1_q[1][:, cols], w1_grouped[0][:, t].rearrange("p m j -> p (m j)"))
+        quantize_pair(w1_q, w1_grouped[1], 1)
         score_kept = sbuf("score_kept", [P, V], F32)
         nc.vector.tensor_copy(score_kept[:], score_sb[:].indirect(kept_sb[:]))
 
         z = sbuf("z", [P, PACK, V], F32)
         h = [sbuf("h%d" % t, [P, S], F32) for t in range(PACK)]
 
-        def hidden(t, cols, bank):
-            h_ps = ps.tile([P, cols.stop - cols.start], F32, name="h_ps", tag="bank%d" % bank)
-            product(h_ps[:], w1_pairs, t, xw[:, cols], xs[:, cols])
-            nc.scalar.activation(h[t][:, cols], h_ps[:], RELU)
-
-        kept_halves = halves_of(V)
-        all_kept = slice(0, V)
+        def hidden(t, cols, b):
+            h_ps = bank(b, "h_ps")
+            product(h_ps[:, 0 : width(cols)], w1_q, t, xw[:, cols], xs[:, cols])
+            nc.scalar.activation(h[t][:, cols], h_ps[:, 0 : width(cols)], RELU)
 
         def weigh(t, entries):
             window = h[t][:].indirect(kept_sb[:, list_columns(entries)])
             nc.vector.tensor_tensor(z[:, t, entries], window, score_kept[:, entries], MULT)
 
-        hidden(0, node_halves[0], bank=0)
-        hidden(1, node_halves[0], bank=1)
-        hidden(0, node_halves[1], bank=2)
-        weigh(0, all_kept)
-        hidden(1, node_halves[1], bank=3)
-        weigh(1, all_kept)
-        hidden(2, slice(0, S), bank=4)
-        weigh(2, all_kept)
-        hidden(3, slice(0, S), bank=5)
-        for entries in kept_halves:
-            weigh(3, entries)
+        for t in range(PACK):
+            for i in range(2):
+                hidden(t, node_halves[i], 2 * t + i)
+            for entries in kept_halves if t == PACK - 1 else [slice(0, V)]:
+                weigh(t, entries)
 
-        half = V // 2
-        w2_grouped = [
-            shared.tile([P, 2, P, PACK], BF16, name="w2_grouped0", offset=0, align_bytes=ALIGN)[:],
-            grouped_pair("w2", 1),
-        ]
-        for pair in range(2):
-            round_pair(w2_grouped[pair], w2_raw, pair, nc.scalar.copy)
-        z_grouped = [
-            sbuf("z_grouped0", [P, half, PACK], BF16),
-            shared.tile([P, half, PACK], BF16, name="z_grouped1", offset=1024, align_bytes=ALIGN),
-        ]
+        w2_q = weight_tiles("w2")
+        w2_grouped = [placed("w2_grouped0", [P, 2, P, PACK], BF16, 0), sbuf("w2_grouped1", [P, 2, P, PACK], BF16)]
+        for i in range(2):
+            round_quarters(nc.scalar.copy, w2_grouped[i], w2_raw, pairs[i], all_places)
+        z_grouped = [sbuf("z_grouped0", [P, half, PACK], BF16), placed("z_grouped1", [P, half, PACK], BF16, 1024)]
         z_codes = sbuf("z_codes", [P, V], U32)
-        z_scales = [
-            shared.tile([P, half], U8, name="z_scales0", offset=0, align_bytes=ALIGN),
-            sbuf("z_scales1", [P, half], U8),
-        ]
-
-        def round_z(i):
+        z_scales = [placed("z_scales0", [P, half], U8, 0), sbuf("z_scales1", [P, half], U8)]
+        for i in range(2):
             interleave(nc.vector.tensor_copy, z_grouped[i][:], z[:, :, kept_halves[i]])
+            quantize_pair(w2_q, w2_grouped[i], i)
+            quantize(z_codes[:, kept_halves[i]], z_scales[i][:], z_grouped[i][:].rearrange("p v t -> p (v t)"))
 
-        def quantize_z(i):
-            nc.vector.quantize_mx(
-                out=z_codes[:, kept_halves[i]].bitcast(FP8X4),
-                scales=z_scales[i][:],
-                in_=z_grouped[i][:].rearrange("p v t -> p (v t)"),
-            )
+        banks = {b: bank(b, "bank") for b in (0, 1, 2, 4, 5, 6, 7)}
 
-        round_z(0)
-        w2_pairs = [quantize_pair("w2", w2_grouped[0], 0)]
-        quantize_z(0)
-        round_z(1)
-        w2_pairs.append(quantize_pair("w2", w2_grouped[1], 1))
-        quantize_z(1)
+        def scatter(t, entries, staged):
+            nc.vector.tensor_copy(up[t][:].indirect(kept_sb[:, list_columns(entries)]), staged)
+
+        def second(b, pieces, staged):
+            for k, (t, i) in enumerate(pieces):
+                product(banks[b][:, kept_halves[k]], w2_q, t, z_codes[:, kept_halves[i]], z_scales[i][:])
+            nc.scalar.copy(staged, banks[b][:, 0 : half * len(pieces)])
+
+        w3_q = weight_tiles("w3")
+        w3_grouped = [sbuf("w3_grouped%d" % i, [P, 2, P, PACK], BF16) for i in range(2)]
+        rr = sbuf("rr", [P, 2 * V], F32)
+        for t in range(2):
+            second(t, [(t, 0)], rr[:, kept_halves[t]])
+            scatter(t, kept_halves[0], rr[:, kept_halves[t]])
+        round_quarters(nc.scalar.copy, w3_grouped[0], w3_raw, pairs[0], all_places)
+        quantize_pair(w3_q, w3_grouped[0], 0)
+        second(2, [(0, 1), (1, 1)], rr[:, V : 2 * V])
+        for t in range(2):
+            scatter(t, kept_halves[1], rr[:, V + t * half : V + (t + 1) * half])
+        round_quarters(nc.scalar.copy, w3_grouped[1], w3_raw, pairs[1], all_places)
+        quantize_pair(w3_q, w3_grouped[1], 1)
 
         result = sbuf("result", [P, PACK, S], F32)
         out_rows = out_0.rearrange("(p t) n -> p t n", t=PACK)
-        banks = {b: ps.tile([P, S], F32, name="bank", tag="bank%d" % b) for b in range(8)}
         y_ps = [banks[6], banks[7], banks[0], banks[1]]
-
-        def put_back(t, halves, bank, staged):
-            entries = slice(kept_halves[halves[0]].start, kept_halves[halves[-1]].stop)
-            for i in halves:
-                cols = slice(kept_halves[i].start - entries.start, kept_halves[i].stop - entries.start)
-                product(banks[bank][:, cols], w2_pairs, t, z_codes[:, kept_halves[i]], z_scales[i][:])
-            nc.scalar.copy(staged, banks[bank][:, 0 : entries.stop - entries.start])
-            nc.vector.tensor_copy(up[t][:].indirect(kept_sb[:, list_columns(entries)]), staged)
-
-        def skip(t):
-            product(y_ps[t][:], w3_pairs, t, xw[:], xs[:])
+        y = [w3_raw[:, 0, :], w3_raw[:, 3, :], w2_raw[:, 2, :]]
 
         def store_quarter(t):
             nc.sync.dma_start(out=out_rows[:, t, :], in_=result[:, t, :])
 
         def add_on_gpsimd(t):
-            y = w2_raw[:, t, :]
-            nc.scalar.copy(y, y_ps[t][:])
-            nc.gpsimd.tensor_tensor(result[:, t, :], up[t][:], y, ADD)
+            product(y_ps[t][:], w3_q, t, xw[:], xs[:])
+            nc.scalar.copy(y[t], y_ps[t][:])
+            nc.gpsimd.tensor_tensor(result[:, t, :], up[t][:], y[t], ADD)
             store_quarter(t)
 
-        rr = sbuf("rr", [P, 3, half], F32)
-        put_back(0, (0,), 0, rr[:, 0, :])
-        put_back(1, (0,), 1, rr[:, 1, :])
-        put_back(0, (1,), 2, rr[:, 2, :])
-        w3_pairs = []
-        for pair in range(2):
-            grouped = round_pair(grouped_pair("w3", pair), w3_raw, pair, nc.scalar.copy, halves_of(P))
-            w3_pairs.append(quantize_pair("w3", grouped, pair))
-        put_back(1, (1,), 3, w3_raw[:, 0, 0:half])
-        put_back(2, (0, 1), 4, w3_raw[:, 1, 0:V])
-        skip(0)
+        second(4, [(2, 0), (2, 1)], w3_raw[:, 1, 0:V])
+        scatter(2, slice(0, V), w3_raw[:, 1, 0:V])
         add_on_gpsimd(0)
-        skip(1)
         add_on_gpsimd(1)
-        put_back(3, (0, 1), 5, w3_raw[:, 2, 0:V])
-        skip(2)
+        second(5, [(3, 0), (3, 1)], w3_raw[:, 2, 0:V])
+        scatter(3, slice(0, V), w3_raw[:, 2, 0:V])
         add_on_gpsimd(2)
-        skip(3)
+        last = PACK - 1
+        y_last = y_ps[last]
+        product(y_last[:], w3_q, last, xw[:], xs[:])
+
         o_scales = sbuf("o_scales", [P, S], U8)
         out_words = out_1[0].rearrange("p n j -> p (n j)").bitcast(I32)
         o_grouped = [sbuf("o_grouped%d" % i, [P, S // 2, PACK], BF16) for i in range(2)]
 
         def interleave_pair(copy, i, cols, pair):
-            quarters = slice(2 * pair, 2 * pair + 2)
             lo = node_halves[i].start
             interleave(
-                copy, o_grouped[i][:, cols, quarters], result[:, quarters, lo + cols.start : lo + cols.stop]
+                copy, o_grouped[i][:, cols, pairs[pair]], result[:, pairs[pair], lo + cols.start : lo + cols.stop]
             )
 
         for i in (1, 0):
             interleave_pair(nc.scalar.copy, i, slice(0, S // 2), 0)
-        last = PACK - 1
         for cols in node_halves:
-            nc.vector.tensor_tensor(result[:, last, cols], up[last][:, cols], y_ps[last][:, cols], ADD)
+            nc.vector.tensor_tensor(result[:, last, cols], up[last][:, cols], y_last[:, cols], ADD)
         store_quarter(last)
         interleave_pair(nc.scalar.copy, 0, slice(0, SCALAR_COLS), 1)
         interleave_pair(nc.vector.tensor_copy, 0, slice(SCALAR_COLS, S // 2), 1)
         interleave_pair(nc.vector.tensor_copy, 1, slice(0, S // 2), 1)
         for i in (0, 1):
             o_codes = sbuf("o_codes%d" % i, [P, S // 2], I32)
-            nc.vector.quantize_mx(
-                out=o_codes[:].bitcast(FP8X4),
-                scales=o_scales[:, node_halves[i]],
-                in_=o_grouped[i][:].rearrange("p n t -> p (n t)"),
-            )
+            quantize(o_codes[:], o_scales[:, node_halves[i]], o_grouped[i][:].rearrange("p n t -> p (n t)"))
             nc.sync.dma_start(out=out_words[:, node_halves[i]], in_=o_codes[:])
         for q in range(P // QUADRANT):
             queue = nc.scalar if q % 2 == 0 else nc.sync

@@ -234,9 +234,8 @@ def tile_picked_ygunet_none_po_kernel(
 
         def interleave_pair(copy, i, cols, pair):
             lo = node_halves[i].start
-            interleave(
-                copy, o_grouped[i][:, cols, pairs[pair]], result[:, pairs[pair], lo + cols.start : lo + cols.stop]
-            )
+            src = result[:, pairs[pair], lo + cols.start : lo + cols.stop]
+            copy(out=o_grouped[i][:, cols, pairs[pair]], in_=src.rearrange("p t c -> p c t"))
 
         for i in (1, 0):
             interleave_pair(nc.scalar.copy, i, slice(0, S // 2), 0)

@@ -139,8 +139,8 @@ def tile_picked_ygunet_none_po_kernel(
             round_half(nc.scalar.copy, w1_grouped, w1_raw, i, 0)
         src = w1_raw[1][:].rearrange("p j (m t) -> p m j t", t=PACK)[:, :, :, pairs[0]]
         dst = w1_grouped[0][:].rearrange("p u m j -> p m j u")[:, place_halves[1]]
-        nc.vector.tensor_copy(out=dst[:, 0:48], in_=src[:, 0:48])
-        nc.scalar.copy(out=dst[:, 48:64], in_=src[:, 48:64])
+        nc.vector.tensor_copy(out=dst[:, 0:16], in_=src[:, 0:16])
+        nc.scalar.copy(out=dst[:, 16:64], in_=src[:, 16:64])
         round_half(nc.scalar.copy, w1_grouped, w1_raw, 1, 1)
         for t in range(2):
             cols = slice(t * P, (t + 1) * P)

@@ -22,6 +22,7 @@ LIST_ROWS = 16
 QUADRANT = 32
 SCALE_ROWS = 4
 LINE = 4
+SPREAD = 8
 SCALAR_COLS = 128
 ALIGN = 64
 
@@ -51,11 +52,6 @@ def tile_picked_ygunet_none_po_kernel(
 
         def bank(b, name):
             return ps.tile([P, S], F32, name=name, tag="bank%d" % b)
-
-        def load_weight(name, w, cols):
-            raw = sbuf(name, [P, PACK, width(cols)], F32)
-            nc.sync.dma_start(out=raw[:], in_=w[:, cols].rearrange("(p j) c -> p j c", j=PACK))
-            return raw
 
         def round_quarters(copy, grouped, raw, quarters, places):
             src = raw[:].rearrange("p j (m t) -> p m j t", t=PACK)[:, places, :, quarters]
@@ -92,60 +88,60 @@ def tile_picked_ygunet_none_po_kernel(
 
         pairs = [slice(0, 2), slice(2, 4)]
         node_halves = [slice(0, S // 2), slice(S // 2, S)]
-        place_halves = [slice(0, P // 2), slice(P // 2, P)]
         all_places = slice(0, P)
 
-        col_halves = [slice(0, H // 2), slice(H // 2, H)]
         kept_halves = [slice(0, V // 2), slice(V // 2, V)]
         half = V // 2
-
-        def round_half(copy, grouped, raw, i, h):
-            src = raw[h][:].rearrange("p j (m t) -> p m j t", t=PACK)[:, :, :, pairs[i]]
-            copy(out=grouped[i][:].rearrange("p u m j -> p m j u")[:, place_halves[h]], in_=src)
 
         def quantize_pair(weight, grouped, i):
             cols = slice(2 * P * i, 2 * P * (i + 1))
             quantize(weight[0][:, cols], weight[1][:, cols], grouped[:].rearrange("p u m j -> p (u m j)"))
 
-        xs_all = sbuf("xs_all", [P, T], U8)
-        nc.vector.memset(xs_all[:].bitcast(I32), 0)
-        xw_all = sbuf("xw_all", [P, T], I32)
-        nc.sync.dma_start(out=xw_all[:], in_=x_words[0].rearrange("p n j -> p (n j)").bitcast(I32))
+        KB = 1024
+        xs_all = placed("xs_all", [P, T], U8, 2 * KB)
+        nc.gpsimd.memset(xs_all[:].bitcast(I32), 0)
+        w1_rows = w1.rearrange("(p j) c -> p j c", j=PACK)
+        w1_raw = placed("w1_raw", [P, PACK, H], F32, 16 * KB)
+        nc.sync.dma_start(out=w1_raw[:, pairs[0], :], in_=w1_rows[:, pairs[0], :])
         offs_sb = sbuf("offs_sb", [P, S // LIST_ROWS], U16)
         nc.sync.dma_start(offs_sb[:], offs)
-        w1_raw = [load_weight("w1_raw0", w1, col_halves[0])]
-        for q in range(P // QUADRANT):
-            in_sbuf, in_dram = scale_rows(xs_all, x_scales, q)
-            nc.sync.dma_start(out=in_sbuf, in_=in_dram)
-        w1_raw.append(load_weight("w1_raw1", w1, col_halves[1]))
+        nc.sync.dma_start(out=xs_all[0:P:SPREAD, :].bitcast(I32), in_=x_scales[0].bitcast(I32))
+        nc.sync.dma_start(out=w1_raw[:, pairs[1], :], in_=w1_rows[:, pairs[1], :])
+        xw_all = sbuf("xw_all", [P, T], I32)
+        nc.sync.dma_start(out=xw_all[:], in_=x_words[0].rearrange("p n j -> p (n j)").bitcast(I32))
         kept_sb = sbuf("kept_sb", [P, V // LIST_ROWS], U16)
         nc.sync.dma_start(kept_sb[:], kept)
         score_sb = sbuf("score_sb", [P, S], F32)
         nc.sync.dma_start(out=score_sb[:], in_=score)
-        w2_raw = load_weight("w2_raw", w2, slice(0, N))
-        w3_raw = load_weight("w3_raw", w3, slice(0, N))
         up = [sbuf("up%d" % t, [P, S], F32) for t in range(PACK)]
         for t in range(PACK):
             nc.vector.memset(up[t][:], 0.0)
 
-        xw = sbuf("xw", [P, S], U32)
-        nc.vector.tensor_copy(xw[:], xw_all[:].bitcast(U32).indirect(offs_sb[:]))
+        xs_spread = sbuf("xs_spread", [P, S], U8)
+        nc.vector.tensor_copy(xs_spread[:], xs_all[:].indirect(offs_sb[:]))
         xs = sbuf("xs", [P, S], U8)
-        nc.vector.tensor_copy(xs[:], xs_all[:].indirect(offs_sb[:]))
+        nc.gpsimd.memset(xs[:].bitcast(I32), 0)
+        for r in range(SCALE_ROWS):
+            nc.sync.dma_start(
+                out=xs[r:P:QUADRANT, :].bitcast(I32), in_=xs_spread[SPREAD * r : P : QUADRANT, :].bitcast(I32)
+            )
+        w2_raw = placed("w2_raw", [P, PACK, N], F32, 2 * KB)
+        nc.sync.dma_start(out=w2_raw[:], in_=w2.rearrange("(p j) c -> p j c", j=PACK))
 
         w1_q = weight_tiles("w1")
         w1_grouped = [sbuf("w1_grouped%d" % i, [P, 2, P, PACK], BF16) for i in range(2)]
+        round_quarters(nc.vector.tensor_copy, w1_grouped[0], w1_raw, pairs[0], all_places)
+        for rows in pairs:
+            src = w1_raw[:, rows, :].rearrange("p j (m t) -> p m j t", t=PACK)[:, :, :, pairs[1]]
+            nc.scalar.copy(out=w1_grouped[1][:, :, :, rows].rearrange("p u m j -> p m j u"), in_=src)
         for i in range(2):
-            round_half(nc.scalar.copy, w1_grouped, w1_raw, i, 0)
-        src = w1_raw[1][:].rearrange("p j (m t) -> p m j t", t=PACK)[:, :, :, pairs[0]]
-        dst = w1_grouped[0][:].rearrange("p u m j -> p m j u")[:, place_halves[1]]
-        nc.vector.tensor_copy(out=dst[:, 0:16], in_=src[:, 0:16])
-        nc.scalar.copy(out=dst[:, 16:64], in_=src[:, 16:64])
-        round_half(nc.scalar.copy, w1_grouped, w1_raw, 1, 1)
-        for t in range(2):
-            cols = slice(t * P, (t + 1) * P)
-            quantize(w1_q[0][:, cols], w1_q[1][:, cols], w1_grouped[0][:, t].rearrange("p m j -> p (m j)"))
-        quantize_pair(w1_q, w1_grouped[1], 1)
+            quantize_pair(w1_q, w1_grouped[i], i)
+
+        xw = sbuf("xw", [P, S], U32)
+        for cols in node_halves:
+            nc.vector.tensor_copy(xw[:, cols], xw_all[:].bitcast(U32).indirect(offs_sb[:, list_columns(cols)]))
+        w3_raw = placed("w3_raw", [P, PACK, N], F32, 16 * KB)
+        nc.sync.dma_start(out=w3_raw[:], in_=w3.rearrange("(p j) c -> p j c", j=PACK))
         score_kept = sbuf("score_kept", [P, V], F32)
         nc.vector.tensor_copy(score_kept[:], score_sb[:].indirect(kept_sb[:]))
 
@@ -161,9 +157,13 @@ def tile_picked_ygunet_none_po_kernel(
             window = h[t][:].indirect(kept_sb[:, list_columns(entries)])
             nc.vector.tensor_tensor(z[:, t, entries], window, score_kept[:, entries], MULT)
 
-        for t in range(PACK):
+        for i in range(2):
+            for t in range(2):
+                hidden(t, node_halves[i], 2 * t + i)
+        for t in range(2, PACK):
             for i in range(2):
                 hidden(t, node_halves[i], 2 * t + i)
+        for t in range(PACK):
             for entries in kept_halves if t == PACK - 1 else [slice(0, V)]:
                 weigh(t, entries)
 

@@ -98,7 +98,7 @@ def tile_picked_ygunet_none_po_kernel(
             quantize(weight[0][:, cols], weight[1][:, cols], grouped[:].rearrange("p u m j -> p (u m j)"))
 
         KB = 1024
-        xs_all = placed("xs_all", [P, T], U8, 2 * KB)
+        xs_all = placed("xs_all", [P, T], U8, 4 * KB)
         nc.gpsimd.memset(xs_all[:].bitcast(I32), 0)
         w1_rows = w1.rearrange("(p j) c -> p j c", j=PACK)
         w1_raw = placed("w1_raw", [P, PACK, H], F32, 16 * KB)
@@ -111,11 +111,9 @@ def tile_picked_ygunet_none_po_kernel(
         nc.sync.dma_start(out=xw_all[:], in_=x_words[0].rearrange("p n j -> p (n j)").bitcast(I32))
         kept_sb = sbuf("kept_sb", [P, V // LIST_ROWS], U16)
         nc.sync.dma_start(kept_sb[:], kept)
-        score_sb = sbuf("score_sb", [P, S], F32)
-        nc.sync.dma_start(out=score_sb[:], in_=score)
         up = [sbuf("up%d" % t, [P, S], F32) for t in range(PACK)]
         for t in range(PACK):
-            nc.vector.memset(up[t][:], 0.0)
+            nc.gpsimd.memset(up[t][:], 0.0)
 
         xs_spread = sbuf("xs_spread", [P, S], U8)
         nc.vector.tensor_copy(xs_spread[:], xs_all[:].indirect(offs_sb[:]))
@@ -125,7 +123,9 @@ def tile_picked_ygunet_none_po_kernel(
             nc.sync.dma_start(
                 out=xs[r:P:QUADRANT, :].bitcast(I32), in_=xs_spread[SPREAD * r : P : QUADRANT, :].bitcast(I32)
             )
-        w2_raw = placed("w2_raw", [P, PACK, N], F32, 2 * KB)
+        score_sb = placed("score_sb", [P, S], F32, 3 * KB)
+        nc.sync.dma_start(out=score_sb[:], in_=score)
+        w2_raw = placed("w2_raw", [P, PACK, N], F32, 5 * KB)
         nc.sync.dma_start(out=w2_raw[:], in_=w2.rearrange("(p j) c -> p j c", j=PACK))
 
         w1_q = weight_tiles("w1")

@@ -118,8 +118,8 @@ def tile_picked_ygunet_none_po_kernel(
         xs_spread = sbuf("xs_spread", [P, S], U8)
         nc.vector.tensor_copy(xs_spread[:], xs_all[:].indirect(offs_sb[:]))
         xs = sbuf("xs", [P, S], U8)
-        nc.gpsimd.memset(xs[:].bitcast(I32), 0)
-        for r in range(SCALE_ROWS):
+        nc.vector.tensor_copy(xs[:].bitcast(I32), xs_spread[:].bitcast(I32))
+        for r in range(1, SCALE_ROWS):
             nc.sync.dma_start(
                 out=xs[r:P:QUADRANT, :].bitcast(I32), in_=xs_spread[SPREAD * r : P : QUADRANT, :].bitcast(I32)
             )
@@ -157,12 +157,17 @@ def tile_picked_ygunet_none_po_kernel(
             window = h[t][:].indirect(kept_sb[:, list_columns(entries)])
             nc.vector.tensor_tensor(z[:, t, entries], window, score_kept[:, entries], MULT)
 
-        for i in range(2):
-            for t in range(2):
-                hidden(t, node_halves[i], 2 * t + i)
+        hidden(0, node_halves[0], 0)
+        early = bank(1, "h_ps")
+        product(early[:, 0:P], w1_q, 1, xw[:, 0:P], xs[:, 0:P])
+        hidden(0, slice(2 * P, 3 * P), 2)
+        hidden(0, slice(3 * P, S), 3)
+        product(early[:, P : 3 * P], w1_q, 1, xw[:, P : 3 * P], xs[:, P : 3 * P])
+        nc.scalar.activation(h[1][:, 0 : 3 * P], early[:, 0 : 3 * P], RELU)
+        hidden(1, slice(3 * P, S), 5)
         for t in range(2, PACK):
             for i in range(2):
-                hidden(t, node_halves[i], 2 * t + i)
+                hidden(t, node_halves[i], (6, 7, 4, 0)[2 * t - 4 + i])
         for t in range(PACK):
             for entries in kept_halves if t == PACK - 1 else [slice(0, V)]:
                 weigh(t, entries)

@@ -137,6 +137,9 @@ def tile_picked_ygunet_none_po_kernel(
         for i in range(2):
             quantize_pair(w1_q, w1_grouped[i], i)
 
+        warm = bank(7, "warm")
+        for t in range(2):
+            product(warm[:], w1_q, t, w1_q[0][:], w1_q[1][:])
         xw = sbuf("xw", [P, S], U32)
         for cols in node_halves:
             nc.vector.tensor_copy(xw[:, cols], xw_all[:].bitcast(U32).indirect(offs_sb[:, list_columns(cols)]))

@@ -13,6 +13,7 @@ U16 = mybir.dt.uint16
 U8 = mybir.dt.uint8
 FP8X4 = mybir.dt.float8_e4m3fn_x4
 RELU = mybir.ActivationFunctionType.Relu
+COPY = mybir.ActivationFunctionType.Copy
 MULT = mybir.AluOpType.mult
 ADD = mybir.AluOpType.add
 
@@ -137,9 +138,6 @@ def tile_picked_ygunet_none_po_kernel(
         for i in range(2):
             quantize_pair(w1_q, w1_grouped[i], i)
 
-        warm = bank(7, "warm")
-        for t in range(2):
-            product(warm[:], w1_q, t, w1_q[0][:], w1_q[1][:])
         xw = sbuf("xw", [P, S], U32)
         for cols in node_halves:
             nc.vector.tensor_copy(xw[:, cols], xw_all[:].bitcast(U32).indirect(offs_sb[:, list_columns(cols)]))
@@ -156,10 +154,6 @@ def tile_picked_ygunet_none_po_kernel(
             product(h_ps[:, 0 : width(cols)], w1_q, t, xw[:, cols], xs[:, cols])
             nc.scalar.activation(h[t][:, cols], h_ps[:, 0 : width(cols)], RELU)
 
-        def weigh(t, entries):
-            window = h[t][:].indirect(kept_sb[:, list_columns(entries)])
-            nc.vector.tensor_tensor(z[:, t, entries], window, score_kept[:, entries], MULT)
-
         hidden(0, node_halves[0], 0)
         early = bank(1, "h_ps")
         product(early[:, 0:P], w1_q, 1, xw[:, 0:P], xs[:, 0:P])
@@ -173,68 +167,70 @@ def tile_picked_ygunet_none_po_kernel(
                 hidden(t, node_halves[i], (6, 7, 4, 0)[2 * t - 4 + i])
         for t in range(PACK):
             for entries in kept_halves if t == PACK - 1 else [slice(0, V)]:
-                weigh(t, entries)
+                window = h[t][:].indirect(kept_sb[:, list_columns(entries)])
+                nc.vector.tensor_tensor(z[:, t, entries], window, score_kept[:, entries], MULT)
 
         w2_q = weight_tiles("w2")
-        w2_grouped = [placed("w2_grouped0", [P, 2, P, PACK], BF16, 0), sbuf("w2_grouped1", [P, 2, P, PACK], BF16)]
+        w2_parts = [slice(0, 1), slice(1, PACK)]
+        w2_grouped = [placed("w2_grouped0", [P, 1, P, PACK], BF16, 0), sbuf("w2_grouped1", [P, PACK - 1, P, PACK], BF16)]
         for i in range(2):
-            round_quarters(nc.scalar.copy, w2_grouped[i], w2_raw, pairs[i], all_places)
-        z_grouped = [sbuf("z_grouped0", [P, half, PACK], BF16), placed("z_grouped1", [P, half, PACK], BF16, 1024)]
+            round_quarters(nc.scalar.copy, w2_grouped[i], w2_raw, w2_parts[i], all_places)
+        z_grouped = [placed("z_grouped0", [P, half, PACK], BF16, KB), sbuf("z_grouped1", [P, half, PACK], BF16)]
         z_codes = sbuf("z_codes", [P, V], U32)
-        z_scales = [placed("z_scales0", [P, half], U8, 0), sbuf("z_scales1", [P, half], U8)]
-        for i in range(2):
-            interleave(nc.vector.tensor_copy, z_grouped[i][:], z[:, :, kept_halves[i]])
-            quantize_pair(w2_q, w2_grouped[i], i)
+        z_scales = [sbuf("z_scales%d" % i, [P, half], U8) for i in range(2)]
+
+        def quantize_z(i):
             quantize(z_codes[:, kept_halves[i]], z_scales[i][:], z_grouped[i][:].rearrange("p v t -> p (v t)"))
 
-        banks = {b: bank(b, "bank") for b in (0, 1, 2, 4, 5, 6, 7)}
+        def quantize_quarters(weight, grouped, quarters):
+            cols = slice(P * quarters.start, P * quarters.stop)
+            quantize(weight[0][:, cols], weight[1][:, cols], grouped[:].rearrange("p u m j -> p (u m j)"))
 
-        def scatter(t, entries, staged):
-            nc.vector.tensor_copy(up[t][:].indirect(kept_sb[:, list_columns(entries)]), staged)
-
-        def second(b, pieces, staged):
-            for k, (t, i) in enumerate(pieces):
-                product(banks[b][:, kept_halves[k]], w2_q, t, z_codes[:, kept_halves[i]], z_scales[i][:])
-            nc.scalar.copy(staged, banks[b][:, 0 : half * len(pieces)])
-
+        quantize_quarters(w2_q, w2_grouped[0], w2_parts[0])
+        for i in range(2):
+            interleave(nc.vector.tensor_copy, z_grouped[i][:], z[:, :, kept_halves[i]])
+        for i in range(2):
+            quantize_z(i)
+        quantize_quarters(w2_q, w2_grouped[1], w2_parts[1])
         w3_q = weight_tiles("w3")
-        w3_grouped = [sbuf("w3_grouped%d" % i, [P, 2, P, PACK], BF16) for i in range(2)]
-        rr = sbuf("rr", [P, 2 * V], F32)
-        for t in range(2):
-            second(t, [(t, 0)], rr[:, kept_halves[t]])
-            scatter(t, kept_halves[0], rr[:, kept_halves[t]])
-        round_quarters(nc.scalar.copy, w3_grouped[0], w3_raw, pairs[0], all_places)
+        w3_grouped = [placed("w3_grouped%d" % i, [P, 2, P, PACK], BF16, 0) if i == 0 else sbuf("w3_grouped1", [P, 2, P, PACK], BF16) for i in range(2)]
+        for i in range(2):
+            round_quarters(nc.vector.tensor_copy, w3_grouped[i], w3_raw, pairs[i], all_places)
         quantize_pair(w3_q, w3_grouped[0], 0)
-        second(2, [(0, 1), (1, 1)], rr[:, V : 2 * V])
-        for t in range(2):
-            scatter(t, kept_halves[1], rr[:, V + t * half : V + (t + 1) * half])
-        round_quarters(nc.scalar.copy, w3_grouped[1], w3_raw, pairs[1], all_places)
+
+        rr = [sbuf("rr%d" % t, [P, V], F32) for t in range(PACK - 1)] + [w3_raw[:, 0, 0:V]]
+
+        def second(copy, b, t, entries):
+            rr_ps = bank(b, "rr_ps")
+            for i in range(entries.start // half, entries.stop // half):
+                product(rr_ps[:, kept_halves[i]], w2_q, t, z_codes[:, kept_halves[i]], z_scales[i][:])
+            copy(rr[t][:, entries], rr_ps[:, entries])
+
+        def scatter_on_scalar(t, entries):
+            nc.scalar.activation(up[t][:].indirect(kept_sb[:, list_columns(entries)]), rr[t][:, entries], COPY)
+
+        def scatter_on_vector(t, entries):
+            nc.vector.tensor_copy(up[t][:].indirect(kept_sb[:, list_columns(entries)]), rr[t][:, entries])
+
+        everyone = slice(0, V)
+        for i in range(2):
+            second(nc.scalar.copy, 1 + i, 0, kept_halves[i])
+            scatter_on_scalar(0, kept_halves[i])
+        for t in (1, 2):
+            second(nc.scalar.copy, 2 + t, t, everyone)
+            scatter_on_scalar(t, everyone)
+        second(nc.vector.tensor_copy, 5, 3, everyone)
         quantize_pair(w3_q, w3_grouped[1], 1)
 
         result = sbuf("result", [P, PACK, S], F32)
         out_rows = out_0.rearrange("(p t) n -> p t n", t=PACK)
-        y_ps = [banks[6], banks[7], banks[0], banks[1]]
-        y = [w3_raw[:, 0, :], w3_raw[:, 3, :], w2_raw[:, 2, :]]
 
-        def store_quarter(t):
+        def add_skip(t, pieces):
+            y_ps = bank((6, 7, 1, 0)[t], "y_ps")
+            product(y_ps[:], w3_q, t, xw[:], xs[:])
+            for cols in pieces:
+                nc.vector.tensor_tensor(result[:, t, cols], up[t][:, cols], y_ps[:, cols], ADD)
             nc.sync.dma_start(out=out_rows[:, t, :], in_=result[:, t, :])
-
-        def add_on_gpsimd(t):
-            product(y_ps[t][:], w3_q, t, xw[:], xs[:])
-            nc.scalar.copy(y[t], y_ps[t][:])
-            nc.gpsimd.tensor_tensor(result[:, t, :], up[t][:], y[t], ADD)
-            store_quarter(t)
-
-        second(4, [(2, 0), (2, 1)], w3_raw[:, 1, 0:V])
-        scatter(2, slice(0, V), w3_raw[:, 1, 0:V])
-        add_on_gpsimd(0)
-        add_on_gpsimd(1)
-        second(5, [(3, 0), (3, 1)], w3_raw[:, 2, 0:V])
-        scatter(3, slice(0, V), w3_raw[:, 2, 0:V])
-        add_on_gpsimd(2)
-        last = PACK - 1
-        y_last = y_ps[last]
-        product(y_last[:], w3_q, last, xw[:], xs[:])
 
         o_scales = sbuf("o_scales", [P, S], U8)
         out_words = out_1[0].rearrange("p n j -> p (n j)").bitcast(I32)
@@ -245,14 +241,14 @@ def tile_picked_ygunet_none_po_kernel(
             src = result[:, pairs[pair], lo + cols.start : lo + cols.stop]
             copy(out=o_grouped[i][:, cols, pairs[pair]], in_=src.rearrange("p t c -> p c t"))
 
-        for i in (1, 0):
+        scatter_on_vector(3, everyone)
+        for t in (0, 1, 3):
+            add_skip(t, [slice(0, S)])
+        for i in range(2):
             interleave_pair(nc.scalar.copy, i, slice(0, S // 2), 0)
-        for cols in node_halves:
-            nc.vector.tensor_tensor(result[:, last, cols], up[last][:, cols], y_last[:, cols], ADD)
-        store_quarter(last)
-        interleave_pair(nc.scalar.copy, 0, slice(0, SCALAR_COLS), 1)
-        interleave_pair(nc.vector.tensor_copy, 0, slice(SCALAR_COLS, S // 2), 1)
-        interleave_pair(nc.vector.tensor_copy, 1, slice(0, S // 2), 1)
+        add_skip(2, node_halves)
+        for i in range(2):
+            interleave_pair(nc.vector.tensor_copy, i, slice(0, S // 2), 1)
         for i in (0, 1):
             o_codes = sbuf("o_codes%d" % i, [P, S // 2], I32)
             quantize(o_codes[:], o_scales[:, node_halves[i]], o_grouped[i][:].rearrange("p n t -> p (n t)"))

@@ -160,7 +160,7 @@ def tile_picked_ygunet_none_po_kernel(
         hidden(0, slice(2 * P, 3 * P), 2)
         hidden(0, slice(3 * P, S), 3)
         product(early[:, P : 3 * P], w1_q, 1, xw[:, P : 3 * P], xs[:, P : 3 * P])
-        nc.scalar.activation(h[1][:, 0 : 3 * P], early[:, 0 : 3 * P], RELU)
+        nc.vector.tensor_scalar_max(h[1][:, 0 : 3 * P], early[:, 0 : 3 * P], 0.0)
         hidden(1, slice(3 * P, S), 5)
         for t in range(2, PACK):
             for i in range(2):
@@ -171,62 +171,54 @@ def tile_picked_ygunet_none_po_kernel(
                 nc.vector.tensor_tensor(z[:, t, entries], window, score_kept[:, entries], MULT)
 
         w2_q = weight_tiles("w2")
-        w2_parts = [slice(0, 1), slice(1, PACK)]
-        w2_grouped = [placed("w2_grouped0", [P, 1, P, PACK], BF16, 0), sbuf("w2_grouped1", [P, PACK - 1, P, PACK], BF16)]
+        w2_grouped = [placed("w2_grouped%d" % i, [P, 2, P, PACK], BF16, (0, 14 * KB)[i]) for i in range(2)]
         for i in range(2):
-            round_quarters(nc.scalar.copy, w2_grouped[i], w2_raw, w2_parts[i], all_places)
-        z_grouped = [placed("z_grouped0", [P, half, PACK], BF16, KB), sbuf("z_grouped1", [P, half, PACK], BF16)]
+            round_quarters(nc.scalar.copy, w2_grouped[i], w2_raw, pairs[i], all_places)
+        z_grouped = [sbuf("z_grouped%d" % i, [P, half, PACK], BF16) for i in range(2)]
         z_codes = sbuf("z_codes", [P, V], U32)
-        z_scales = [sbuf("z_scales%d" % i, [P, half], U8) for i in range(2)]
+        z_scales = [sbuf("z_scales0", [P, half], U8), placed("z_scales1", [P, half], U8, 0)]
 
         def quantize_z(i):
             quantize(z_codes[:, kept_halves[i]], z_scales[i][:], z_grouped[i][:].rearrange("p v t -> p (v t)"))
 
-        def quantize_quarters(weight, grouped, quarters):
-            cols = slice(P * quarters.start, P * quarters.stop)
-            quantize(weight[0][:, cols], weight[1][:, cols], grouped[:].rearrange("p u m j -> p (u m j)"))
-
-        quantize_quarters(w2_q, w2_grouped[0], w2_parts[0])
         for i in range(2):
             interleave(nc.vector.tensor_copy, z_grouped[i][:], z[:, :, kept_halves[i]])
         for i in range(2):
             quantize_z(i)
-        quantize_quarters(w2_q, w2_grouped[1], w2_parts[1])
+            quantize_pair(w2_q, w2_grouped[i], i)
         w3_q = weight_tiles("w3")
-        w3_grouped = [placed("w3_grouped%d" % i, [P, 2, P, PACK], BF16, 0) if i == 0 else sbuf("w3_grouped1", [P, 2, P, PACK], BF16) for i in range(2)]
+        w3_grouped = [placed("w3_grouped%d" % i, [P, 2, P, PACK], BF16, (KB // 2, 14 * KB)[i]) for i in range(2)]
         for i in range(2):
             round_quarters(nc.vector.tensor_copy, w3_grouped[i], w3_raw, pairs[i], all_places)
         quantize_pair(w3_q, w3_grouped[0], 0)
 
-        rr = [sbuf("rr%d" % t, [P, V], F32) for t in range(PACK - 1)] + [w3_raw[:, 0, 0:V]]
+        rr = sbuf("rr", [P, PACK, V], F32)
 
-        def second(copy, b, t, entries):
+        def second(copy, b, pieces):
             rr_ps = bank(b, "rr_ps")
-            for i in range(entries.start // half, entries.stop // half):
-                product(rr_ps[:, kept_halves[i]], w2_q, t, z_codes[:, kept_halves[i]], z_scales[i][:])
-            copy(rr[t][:, entries], rr_ps[:, entries])
+            for k, (t, i) in enumerate(pieces):
+                product(rr_ps[:, k * half : (k + 1) * half], w2_q, t, z_codes[:, kept_halves[i]], z_scales[i][:])
+            lo = pieces[0][0] * V + pieces[0][1] * half
+            copy(rr[:].rearrange("p t v -> p (t v)")[:, lo : lo + half * len(pieces)], rr_ps[:, 0 : half * len(pieces)])
 
         def scatter_on_scalar(t, entries):
-            nc.scalar.activation(up[t][:].indirect(kept_sb[:, list_columns(entries)]), rr[t][:, entries], COPY)
-
-        def scatter_on_vector(t, entries):
-            nc.vector.tensor_copy(up[t][:].indirect(kept_sb[:, list_columns(entries)]), rr[t][:, entries])
+            nc.scalar.activation(up[t][:].indirect(kept_sb[:, list_columns(entries)]), rr[:, t, entries], COPY)
 
         everyone = slice(0, V)
-        for i in range(2):
-            second(nc.scalar.copy, 1 + i, 0, kept_halves[i])
-            scatter_on_scalar(0, kept_halves[i])
-        for t in (1, 2):
-            second(nc.scalar.copy, 2 + t, t, everyone)
-            scatter_on_scalar(t, everyone)
-        second(nc.vector.tensor_copy, 5, 3, everyone)
+        second(nc.scalar.copy, 1, [(0, 0)])
+        scatter_on_scalar(0, kept_halves[0])
+        second(nc.scalar.copy, 2, [(0, 1), (1, 0), (1, 1)])
+        scatter_on_scalar(1, everyone)
+        scatter_on_scalar(0, kept_halves[1])
+        second(nc.vector.tensor_copy, 3, [(2, 0), (2, 1), (3, 0), (3, 1)])
+        scatter_on_scalar(2, everyone)
         quantize_pair(w3_q, w3_grouped[1], 1)
 
         result = sbuf("result", [P, PACK, S], F32)
         out_rows = out_0.rearrange("(p t) n -> p t n", t=PACK)
 
         def add_skip(t, pieces):
-            y_ps = bank((6, 7, 1, 0)[t], "y_ps")
+            y_ps = bank((6, 7, 5, 4)[t], "y_ps")
             product(y_ps[:], w3_q, t, xw[:], xs[:])
             for cols in pieces:
                 nc.vector.tensor_tensor(result[:, t, cols], up[t][:, cols], y_ps[:, cols], ADD)
@@ -241,8 +233,8 @@ def tile_picked_ygunet_none_po_kernel(
             src = result[:, pairs[pair], lo + cols.start : lo + cols.stop]
             copy(out=o_grouped[i][:, cols, pairs[pair]], in_=src.rearrange("p t c -> p c t"))
 
-        scatter_on_vector(3, everyone)
-        for t in (0, 1, 3):
+        nc.vector.tensor_copy(up[3][:].indirect(kept_sb[:]), rr[:, 3, :])
+        for t in (1, 3, 0):
             add_skip(t, [slice(0, S)])
         for i in range(2):
             interleave_pair(nc.scalar.copy, i, slice(0, S // 2), 0)

@@ -110,6 +110,8 @@ def tile_picked_ygunet_none_po_kernel(
         nc.sync.dma_start(out=w1_raw[:, pairs[1], :], in_=w1_rows[:, pairs[1], :])
         xw_all = sbuf("xw_all", [P, T], I32)
         nc.sync.dma_start(out=xw_all[:], in_=x_words[0].rearrange("p n j -> p (n j)").bitcast(I32))
+        score_sb = sbuf("score_sb", [P, S], F32)
+        nc.sync.dma_start(out=score_sb[:], in_=score)
         kept_sb = sbuf("kept_sb", [P, V // LIST_ROWS], U16)
         nc.sync.dma_start(kept_sb[:], kept)
         up = [sbuf("up%d" % t, [P, S], F32) for t in range(PACK)]
@@ -124,8 +126,6 @@ def tile_picked_ygunet_none_po_kernel(
             nc.sync.dma_start(
                 out=xs[r:P:QUADRANT, :].bitcast(I32), in_=xs_spread[SPREAD * r : P : QUADRANT, :].bitcast(I32)
             )
-        score_sb = placed("score_sb", [P, S], F32, 3 * KB)
-        nc.sync.dma_start(out=score_sb[:], in_=score)
         w2_raw = placed("w2_raw", [P, PACK, N], F32, 5 * KB)
         nc.sync.dma_start(out=w2_raw[:], in_=w2.rearrange("(p j) c -> p j c", j=PACK))
 
@@ -149,19 +149,19 @@ def tile_picked_ygunet_none_po_kernel(
         z = sbuf("z", [P, PACK, V], F32)
         h = [sbuf("h%d" % t, [P, S], F32) for t in range(PACK)]
 
-        def hidden(t, cols, b):
+        def hidden(t, cols, b, on_vector=False):
             h_ps = bank(b, "h_ps")
             product(h_ps[:, 0 : width(cols)], w1_q, t, xw[:, cols], xs[:, cols])
-            nc.scalar.activation(h[t][:, cols], h_ps[:, 0 : width(cols)], RELU)
+            if on_vector:
+                nc.vector.tensor_scalar_max(h[t][:, cols], h_ps[:, 0 : width(cols)], 0.0)
+            else:
+                nc.scalar.activation(h[t][:, cols], h_ps[:, 0 : width(cols)], RELU)
 
         hidden(0, node_halves[0], 0)
-        early = bank(1, "h_ps")
-        product(early[:, 0:P], w1_q, 1, xw[:, 0:P], xs[:, 0:P])
+        hidden(1, node_halves[0], 1, on_vector=True)
         hidden(0, slice(2 * P, 3 * P), 2)
         hidden(0, slice(3 * P, S), 3)
-        product(early[:, P : 3 * P], w1_q, 1, xw[:, P : 3 * P], xs[:, P : 3 * P])
-        nc.vector.tensor_scalar_max(h[1][:, 0 : 3 * P], early[:, 0 : 3 * P], 0.0)
-        hidden(1, slice(3 * P, S), 5)
+        hidden(1, node_halves[1], 5)
         for t in range(2, PACK):
             for i in range(2):
                 hidden(t, node_halves[i], (6, 7, 4, 0)[2 * t - 4 + i])
@@ -207,9 +207,10 @@ def tile_picked_ygunet_none_po_kernel(
         everyone = slice(0, V)
         second(nc.scalar.copy, 1, [(0, 0)])
         scatter_on_scalar(0, kept_halves[0])
-        second(nc.scalar.copy, 2, [(0, 1), (1, 0), (1, 1)])
-        scatter_on_scalar(1, everyone)
+        second(nc.scalar.copy, 2, [(0, 1)])
+        second(nc.scalar.copy, 0, [(1, 0), (1, 1)])
         scatter_on_scalar(0, kept_halves[1])
+        scatter_on_scalar(1, everyone)
         second(nc.vector.tensor_copy, 3, [(2, 0), (2, 1), (3, 0), (3, 1)])
         scatter_on_scalar(2, everyone)
         quantize_pair(w3_q, w3_grouped[1], 1)
@@ -234,7 +235,7 @@ def tile_picked_ygunet_none_po_kernel(
             copy(out=o_grouped[i][:, cols, pairs[pair]], in_=src.rearrange("p t c -> p c t"))
 
         nc.vector.tensor_copy(up[3][:].indirect(kept_sb[:]), rr[:, 3, :])
-        for t in (1, 3, 0):
+        for t in (0, 1, 3):
             add_skip(t, [slice(0, S)])
         for i in range(2):
             interleave_pair(nc.scalar.copy, i, slice(0, S // 2), 0)

@@ -171,7 +171,7 @@ def tile_picked_ygunet_none_po_kernel(
                 nc.vector.tensor_tensor(z[:, t, entries], window, score_kept[:, entries], MULT)
 
         w2_q = weight_tiles("w2")
-        w2_grouped = [placed("w2_grouped%d" % i, [P, 2, P, PACK], BF16, (0, 14 * KB)[i]) for i in range(2)]
+        w2_grouped = [placed("w2_grouped%d" % i, [P, 2, P, PACK], BF16, (0, 26 * KB)[i]) for i in range(2)]
         for i in range(2):
             round_quarters(nc.scalar.copy, w2_grouped[i], w2_raw, pairs[i], all_places)
         z_grouped = [sbuf("z_grouped%d" % i, [P, half, PACK], BF16) for i in range(2)]
@@ -186,41 +186,48 @@ def tile_picked_ygunet_none_po_kernel(
         for i in range(2):
             quantize_z(i)
             quantize_pair(w2_q, w2_grouped[i], i)
-        w3_q = weight_tiles("w3")
-        w3_grouped = [placed("w3_grouped%d" % i, [P, 2, P, PACK], BF16, (KB // 2, 14 * KB)[i]) for i in range(2)]
-        for i in range(2):
-            round_quarters(nc.vector.tensor_copy, w3_grouped[i], w3_raw, pairs[i], all_places)
-        quantize_pair(w3_q, w3_grouped[0], 0)
+        w3_grouped = [placed("w3_grouped%d" % i, [P, 2, P, PACK], BF16, (24 * KB, 25 * KB)[i]) for i in range(2)]
+        w3_codes = [sbuf("w3_codes%d" % i, [P, 2 * P], U32) for i in range(2)]
+        rr = sbuf("rr", [P, PACK - 1, V], F32)
+        rr_last = sbuf("rr_last", [P, V], F32)
 
-        rr = sbuf("rr", [P, PACK, V], F32)
-
-        def second(copy, b, pieces):
+        def second(copy, b, pieces, staged):
             rr_ps = bank(b, "rr_ps")
             for k, (t, i) in enumerate(pieces):
                 product(rr_ps[:, k * half : (k + 1) * half], w2_q, t, z_codes[:, kept_halves[i]], z_scales[i][:])
-            lo = pieces[0][0] * V + pieces[0][1] * half
-            copy(rr[:].rearrange("p t v -> p (t v)")[:, lo : lo + half * len(pieces)], rr_ps[:, 0 : half * len(pieces)])
+            copy(staged, rr_ps[:, 0 : half * len(pieces)])
 
         def scatter_on_scalar(t, entries):
             nc.scalar.activation(up[t][:].indirect(kept_sb[:, list_columns(entries)]), rr[:, t, entries], COPY)
 
+        def round_on_gpsimd(out, in_):
+            nc.gpsimd.tensor_scalar(out, in_, 1.0, 0.0, MULT, ADD)
+
         everyone = slice(0, V)
-        second(nc.scalar.copy, 1, [(0, 0)])
-        scatter_on_scalar(0, kept_halves[0])
-        second(nc.scalar.copy, 2, [(0, 1)])
-        second(nc.scalar.copy, 0, [(1, 0), (1, 1)])
+        round_quarters(nc.vector.tensor_copy, w3_grouped[0], w3_raw, pairs[0], all_places)
+        for i in range(2):
+            second(nc.scalar.copy, 1 + i, [(0, i)], rr[:, 0, kept_halves[i]])
+            if i == 0:
+                scatter_on_scalar(0, kept_halves[0])
+        second(nc.scalar.copy, 0, [(1, 0), (1, 1)], rr[:, 1, :])
         scatter_on_scalar(0, kept_halves[1])
         scatter_on_scalar(1, everyone)
-        second(nc.vector.tensor_copy, 3, [(2, 0), (2, 1), (3, 0), (3, 1)])
+        second(nc.vector.tensor_copy, 3, [(3, 0), (3, 1)], rr_last[:])
+        w3_scales = [sbuf("w3_scales%d" % i, [P, 2 * P], U8) for i in range(2)]
+        quantize(w3_codes[0][:], w3_scales[0][:], w3_grouped[0][:].rearrange("p u m j -> p (u m j)"))
+        src = w3_raw[:].rearrange("p j (m t) -> p m t j", t=PACK)[:, :, pairs[1], :]
+        round_on_gpsimd(w3_grouped[1][:].rearrange("p u m j -> p m u j"), src)
+        second(nc.vector.tensor_copy, 1, [(2, 0), (2, 1)], rr[:, 2, :])
         scatter_on_scalar(2, everyone)
-        quantize_pair(w3_q, w3_grouped[1], 1)
 
-        result = sbuf("result", [P, PACK, S], F32)
+        nc.vector.tensor_copy(up[3][:].indirect(kept_sb[:]), rr_last[:])
+        quantize(w3_codes[1][:], w3_scales[1][:], w3_grouped[1][:].rearrange("p u m j -> p (u m j)"))
+        result = placed("result", [P, PACK, S], F32, 25 * KB)
         out_rows = out_0.rearrange("(p t) n -> p t n", t=PACK)
 
         def add_skip(t, pieces):
             y_ps = bank((6, 7, 5, 4)[t], "y_ps")
-            product(y_ps[:], w3_q, t, xw[:], xs[:])
+            product(y_ps[:], (w3_codes[t // 2], w3_scales[t // 2]), t % 2, xw[:], xs[:])
             for cols in pieces:
                 nc.vector.tensor_tensor(result[:, t, cols], up[t][:, cols], y_ps[:, cols], ADD)
             nc.sync.dma_start(out=out_rows[:, t, :], in_=result[:, t, :])
@@ -234,7 +241,6 @@ def tile_picked_ygunet_none_po_kernel(
             src = result[:, pairs[pair], lo + cols.start : lo + cols.stop]
             copy(out=o_grouped[i][:, cols, pairs[pair]], in_=src.rearrange("p t c -> p c t"))
 
-        nc.vector.tensor_copy(up[3][:].indirect(kept_sb[:]), rr[:, 3, :])
         for t in (0, 1, 3):
             add_skip(t, [slice(0, S)])
         for i in range(2):

from contextlib import ExitStack

import concourse.mybir as mybir

K, T, S, H, N, V = 512, 2048, 512, 512, 512, 256
FLOPS = 2 * K * H * S + 2 * H * N * V + 2 * K * N * S

F32 = mybir.dt.float32
BF16 = mybir.dt.bfloat16
I32 = mybir.dt.int32
U32 = mybir.dt.uint32
U16 = mybir.dt.uint16
U8 = mybir.dt.uint8
FP8X4 = mybir.dt.float8_e4m3fn_x4
RELU = mybir.ActivationFunctionType.Relu
COPY = mybir.ActivationFunctionType.Copy
MULT = mybir.AluOpType.mult
ADD = mybir.AluOpType.add

P = 128
PACK = 4
LIST_ROWS = 16
QUADRANT = 32
SCALE_ROWS = 4
LINE = 4
SPREAD = 8
SCALAR_COLS = 128
ALIGN = 64


def list_columns(entries):
    return slice(entries.start // LIST_ROWS, entries.stop // LIST_ROWS)


def width(cols):
    return cols.stop - cols.start


def tile_picked_ygunet_none_po_kernel(
    tc, x_words, x_scales, w1, w2, w3, score, offs, kept, out_0, out_1, out_2
):
    nc = tc.nc
    with ExitStack() as ctx:
        sb = ctx.enter_context(tc.tile_pool(name="sb", bufs=1))
        ps = ctx.enter_context(tc.psum_pool(name="ps", bufs=1))
        shared = ctx.enter_context(tc.tile_pool(name="shared", bufs=1))

        def sbuf(name, shape, dtype):
            return sb.tile(shape, dtype, name=name, tag=name, align_bytes=ALIGN)

        def placed(name, shape, dtype, offset):
            return shared.tile(shape, dtype, name=name, offset=offset, align_bytes=ALIGN)

        def bank(b, name):
            return ps.tile([P, S], F32, name=name, tag="bank%d" % b)

        def round_quarters(copy, grouped, raw, quarters, places):
            src = raw[:].rearrange("p j (m t) -> p m j t", t=PACK)[:, places, :, quarters]
            copy(out=grouped[:].rearrange("p u m j -> p m j u")[:, places], in_=src)

        def quantize(codes, scales, grouped):
            nc.vector.quantize_mx(out=codes.bitcast(FP8X4), scales=scales, in_=grouped)

        def weight_tiles(name):
            return sbuf(name + "_codes", [P, PACK * P], U32), sbuf(name + "_scales", [P, PACK * P], U8)

        def product(out, weight, t, codes, scales):
            cols = slice(t * P, (t + 1) * P)
            nc.tensor.matmul_mx(
                out=out,
                lhsT=weight[0][:, cols].bitcast(FP8X4),
                lhsT_scale=weight[1][:, cols],
                rhs=codes.bitcast(FP8X4),
                rhs_scale=scales,
                start=True,
                stop=True,
            )

        def interleave(copy, dst, src):
            copy(
                out=dst.rearrange("p (c i) t -> p c t i", i=LINE),
                in_=src.rearrange("p t (c i) -> p c t i", i=LINE),
            )

        def scale_rows(tile, dram, q):
            in_sbuf = tile[q:P:QUADRANT, :]
            in_dram = dram[0, q : SCALE_ROWS * (P // QUADRANT) : SCALE_ROWS, :]
            return in_sbuf.bitcast(I32), in_dram.bitcast(I32)

        pairs = [slice(0, 2), slice(2, 4)]
        node_halves = [slice(0, S // 2), slice(S // 2, S)]
        all_places = slice(0, P)

        kept_halves = [slice(0, V // 2), slice(V // 2, V)]
        half = V // 2

        def quantize_pair(weight, grouped, i):
            cols = slice(2 * P * i, 2 * P * (i + 1))
            quantize(weight[0][:, cols], weight[1][:, cols], grouped[:].rearrange("p u m j -> p (u m j)"))

        KB = 1024
        xs_all = placed("xs_all", [P, T], U8, 4 * KB)
        nc.gpsimd.memset(xs_all[:].bitcast(I32), 0)
        w1_rows = w1.rearrange("(p j) c -> p j c", j=PACK)
        w1_raw = placed("w1_raw", [P, PACK, H], F32, 16 * KB)
        nc.sync.dma_start(out=w1_raw[:, pairs[0], :], in_=w1_rows[:, pairs[0], :])
        offs_sb = sbuf("offs_sb", [P, S // LIST_ROWS], U16)
        nc.sync.dma_start(offs_sb[:], offs)
        nc.sync.dma_start(out=xs_all[0:P:SPREAD, :].bitcast(I32), in_=x_scales[0].bitcast(I32))
        nc.sync.dma_start(out=w1_raw[:, pairs[1], :], in_=w1_rows[:, pairs[1], :])
        xw_all = sbuf("xw_all", [P, T], I32)
        nc.sync.dma_start(out=xw_all[:], in_=x_words[0].rearrange("p n j -> p (n j)").bitcast(I32))
        score_sb = sbuf("score_sb", [P, S], F32)
        nc.sync.dma_start(out=score_sb[:], in_=score)
        kept_sb = sbuf("kept_sb", [P, V // LIST_ROWS], U16)
        nc.sync.dma_start(kept_sb[:], kept)
        up = [sbuf("up%d" % t, [P, S], F32) for t in range(PACK)]
        for t in range(PACK):
            nc.gpsimd.memset(up[t][:], 0.0)

        xs_spread = sbuf("xs_spread", [P, S], U8)
        nc.vector.tensor_copy(xs_spread[:], xs_all[:].indirect(offs_sb[:]))
        xs = sbuf("xs", [P, S], U8)
        nc.vector.tensor_copy(xs[:].bitcast(I32), xs_spread[:].bitcast(I32))
        for r in range(1, SCALE_ROWS):
            nc.sync.dma_start(
                out=xs[r:P:QUADRANT, :].bitcast(I32), in_=xs_spread[SPREAD * r : P : QUADRANT, :].bitcast(I32)
            )
        w2_raw = placed("w2_raw", [P, PACK, N], F32, 5 * KB)
        nc.sync.dma_start(out=w2_raw[:], in_=w2.rearrange("(p j) c -> p j c", j=PACK))

        w1_q = weight_tiles("w1")
        w1_grouped = [sbuf("w1_grouped%d" % i, [P, 2, P, PACK], BF16) for i in range(2)]
        round_quarters(nc.vector.tensor_copy, w1_grouped[0], w1_raw, pairs[0], all_places)
        for rows in pairs:
            src = w1_raw[:, rows, :].rearrange("p j (m t) -> p m j t", t=PACK)[:, :, :, pairs[1]]
            nc.scalar.copy(out=w1_grouped[1][:, :, :, rows].rearrange("p u m j -> p m j u"), in_=src)
        for i in range(2):
            quantize_pair(w1_q, w1_grouped[i], i)

        xw = sbuf("xw", [P, S], U32)
        for cols in node_halves:
            nc.vector.tensor_copy(xw[:, cols], xw_all[:].bitcast(U32).indirect(offs_sb[:, list_columns(cols)]))
        w3_raw = placed("w3_raw", [P, PACK, N], F32, 16 * KB)
        nc.sync.dma_start(out=w3_raw[:], in_=w3.rearrange("(p j) c -> p j c", j=PACK))
        score_kept = sbuf("score_kept", [P, V], F32)
        nc.vector.tensor_copy(score_kept[:], score_sb[:].indirect(kept_sb[:]))

        z = sbuf("z", [P, PACK, V], F32)
        h = [sbuf("h%d" % t, [P, S], F32) for t in range(PACK)]

        def hidden(t, cols, b, on_vector=False):
            h_ps = bank(b, "h_ps")
            product(h_ps[:, 0 : width(cols)], w1_q, t, xw[:, cols], xs[:, cols])
            if on_vector:
                nc.vector.tensor_scalar_max(h[t][:, cols], h_ps[:, 0 : width(cols)], 0.0)
            else:
                nc.scalar.activation(h[t][:, cols], h_ps[:, 0 : width(cols)], RELU)

        hidden(0, node_halves[0], 0)
        hidden(1, node_halves[0], 1, on_vector=True)
        hidden(0, slice(2 * P, 3 * P), 2)
        hidden(0, slice(3 * P, S), 3)
        hidden(1, node_halves[1], 5)
        for t in range(2, PACK):
            for i in range(2):
                hidden(t, node_halves[i], (6, 7, 4, 0)[2 * t - 4 + i])
        for t in range(PACK):
            for entries in kept_halves if t == PACK - 1 else [slice(0, V)]:
                window = h[t][:].indirect(kept_sb[:, list_columns(entries)])
                nc.vector.tensor_tensor(z[:, t, entries], window, score_kept[:, entries], MULT)

        w2_q = weight_tiles("w2")
        w2_grouped = [placed("w2_grouped%d" % i, [P, 2, P, PACK], BF16, (0, 26 * KB)[i]) for i in range(2)]
        for i in range(2):
            round_quarters(nc.scalar.copy, w2_grouped[i], w2_raw, pairs[i], all_places)
        z_grouped = [sbuf("z_grouped%d" % i, [P, half, PACK], BF16) for i in range(2)]
        z_codes = sbuf("z_codes", [P, V], U32)
        z_scales = [sbuf("z_scales0", [P, half], U8), placed("z_scales1", [P, half], U8, 0)]

        def quantize_z(i):
            quantize(z_codes[:, kept_halves[i]], z_scales[i][:], z_grouped[i][:].rearrange("p v t -> p (v t)"))

        for i in range(2):
            interleave(nc.vector.tensor_copy, z_grouped[i][:], z[:, :, kept_halves[i]])
        for i in range(2):
            quantize_z(i)
            quantize_pair(w2_q, w2_grouped[i], i)
        w3_grouped = [placed("w3_grouped%d" % i, [P, 2, P, PACK], BF16, (24 * KB, 25 * KB)[i]) for i in range(2)]
        w3_codes = [sbuf("w3_codes%d" % i, [P, 2 * P], U32) for i in range(2)]
        rr = sbuf("rr", [P, PACK - 1, V], F32)
        rr_last = sbuf("rr_last", [P, V], F32)

        def second(copy, b, pieces, staged):
            rr_ps = bank(b, "rr_ps")
            for k, (t, i) in enumerate(pieces):
                product(rr_ps[:, k * half : (k + 1) * half], w2_q, t, z_codes[:, kept_halves[i]], z_scales[i][:])
            copy(staged, rr_ps[:, 0 : half * len(pieces)])

        def scatter_on_scalar(t, entries):
            nc.scalar.activation(up[t][:].indirect(kept_sb[:, list_columns(entries)]), rr[:, t, entries], COPY)

        def round_on_gpsimd(out, in_):
            nc.gpsimd.tensor_scalar(out, in_, 1.0, 0.0, MULT, ADD)

        everyone = slice(0, V)
        round_quarters(nc.vector.tensor_copy, w3_grouped[0], w3_raw, pairs[0], all_places)
        for i in range(2):
            second(nc.scalar.copy, 1 + i, [(0, i)], rr[:, 0, kept_halves[i]])
            if i == 0:
                scatter_on_scalar(0, kept_halves[0])
        second(nc.scalar.copy, 0, [(1, 0), (1, 1)], rr[:, 1, :])
        scatter_on_scalar(0, kept_halves[1])
        scatter_on_scalar(1, everyone)
        second(nc.vector.tensor_copy, 3, [(3, 0), (3, 1)], rr_last[:])
        w3_scales = [sbuf("w3_scales%d" % i, [P, 2 * P], U8) for i in range(2)]
        quantize(w3_codes[0][:], w3_scales[0][:], w3_grouped[0][:].rearrange("p u m j -> p (u m j)"))
        src = w3_raw[:].rearrange("p j (m t) -> p m t j", t=PACK)[:, :, pairs[1], :]
        round_on_gpsimd(w3_grouped[1][:].rearrange("p u m j -> p m u j"), src)
        second(nc.vector.tensor_copy, 1, [(2, 0), (2, 1)], rr[:, 2, :])
        scatter_on_scalar(2, everyone)

        nc.vector.tensor_copy(up[3][:].indirect(kept_sb[:]), rr_last[:])
        quantize(w3_codes[1][:], w3_scales[1][:], w3_grouped[1][:].rearrange("p u m j -> p (u m j)"))
        result = placed("result", [P, PACK, S], F32, 25 * KB)
        out_rows = out_0.rearrange("(p t) n -> p t n", t=PACK)

        def add_skip(t, pieces):
            y_ps = bank((6, 7, 5, 4)[t], "y_ps")
            product(y_ps[:], (w3_codes[t // 2], w3_scales[t // 2]), t % 2, xw[:], xs[:])
            for cols in pieces:
                nc.vector.tensor_tensor(result[:, t, cols], up[t][:, cols], y_ps[:, cols], ADD)
            nc.sync.dma_start(out=out_rows[:, t, :], in_=result[:, t, :])

        o_scales = sbuf("o_scales", [P, S], U8)
        out_words = out_1[0].rearrange("p n j -> p (n j)").bitcast(I32)
        o_grouped = [sbuf("o_grouped%d" % i, [P, S // 2, PACK], BF16) for i in range(2)]

        def interleave_pair(copy, i, cols, pair):
            lo = node_halves[i].start
            src = result[:, pairs[pair], lo + cols.start : lo + cols.stop]
            copy(out=o_grouped[i][:, cols, pairs[pair]], in_=src.rearrange("p t c -> p c t"))

        for t in (0, 1, 3):
            add_skip(t, [slice(0, S)])
        for i in range(2):
            interleave_pair(nc.scalar.copy, i, slice(0, S // 2), 0)
        add_skip(2, node_halves)
        for i in range(2):
            interleave_pair(nc.vector.tensor_copy, i, slice(0, S // 2), 1)
        for i in (0, 1):
            o_codes = sbuf("o_codes%d" % i, [P, S // 2], I32)
            quantize(o_codes[:], o_scales[:, node_halves[i]], o_grouped[i][:].rearrange("p n t -> p (n t)"))
            nc.sync.dma_start(out=out_words[:, node_halves[i]], in_=o_codes[:])
        for q in range(P // QUADRANT):
            queue = nc.scalar if q % 2 == 0 else nc.sync
            in_sbuf, in_dram = scale_rows(o_scales, out_2, q)
            queue.dma_start(out=in_dram, in_=in_sbuf)
